import numpy as np
import ml_dtypes


def mxq(x, axis, fmt="e4m3"):
    dtype, down = {"e4m3": (ml_dtypes.float8_e4m3fn, 7), "e5m2": (ml_dtypes.float8_e5m2, 14)}[fmt]
    v = np.moveaxis(np.asarray(x, np.float32).astype(ml_dtypes.bfloat16).astype(np.float64), axis, -1)
    blocks = v.reshape(v.shape[:-1] + (-1, 32))
    amax = np.abs(blocks).max(-1, keepdims=True)
    byte = np.maximum(np.where(amax > 0, np.frexp(amax)[1] - 1 + 127, 0) - down, 1)
    scale = np.exp2(byte - 127.0)
    codes = (blocks / scale).astype(np.float32).astype(dtype).astype(np.float64)
    return np.moveaxis((codes * scale).reshape(v.shape), -1, axis)


WIDE = False


def mx_kscale(k):
    if not WIDE:
        return np.ones(k)
    levels = np.array([10, -10, 5, -5, 0])
    if k % 512:
        return np.exp2(np.random.permutation(np.resize(levels, k // 32))).repeat(32)
    a = np.empty((k // 512, 16))
    for p in range(k // 512):
        a[p, :8] = np.random.permutation(np.resize(levels, 8))
        for g in range(8):
            far = levels[np.abs(levels - a[p, g]) >= 10]
            a[p, g + 8] = far[np.random.randint(len(far))]
    return np.exp2(a.ravel()).repeat(32)


def f64(x):
    return np.asarray(x).astype(np.float64)


def striped(idx):
    return np.tile(idx.reshape(-1, 16).T, (8, 1)).astype(np.uint16)


def unstriped(offs):
    return offs[:16].T.reshape(-1).astype(np.int64)


E2M1 = np.array([0.0, 0.5, 1.0, 1.5, 2.0, 3.0, 4.0, 6.0, -0.0, -0.5, -1.0, -1.5, -2.0, -3.0, -4.0, -6.0])


def pack_weight(w, fmt):
    k, n = w.shape
    w = f64(np.asarray(w, np.float32).astype(ml_dtypes.bfloat16)).reshape(k // 32, 32, n)
    amax = np.abs(w).max(1)
    if fmt == "e4m3":
        byte = np.frexp(amax)[1] - 1 + 127 - 7
    else:
        mant, ex = np.frexp(amax / 6.0)
        byte = np.where(mant > 0.5, ex, ex - 1) + 127
    byte = np.clip(np.where(amax > 0, byte, 1), 1, 254)
    scaled = (w * np.exp2(127.0 - byte)[:, None, :]).reshape(k, n).astype(np.float32)
    by_word = np.ascontiguousarray(scaled.reshape(k // 512, 128, 4, n).transpose(0, 1, 3, 2))
    if fmt == "e4m3":
        words = by_word.astype(ml_dtypes.float8_e4m3fn).view(np.uint8)
    else:
        c = by_word.astype(ml_dtypes.float4_e2m1fn).view(np.uint8) & 0xF
        words = (c[..., 0::2] | (c[..., 1::2] << 4)).reshape(k // 512, 128, 2 * n)
    return np.ascontiguousarray(words), np.ascontiguousarray(byte.astype(np.uint8).reshape(k // 512, 16, n))


def unpack_weight(words, scales, fmt):
    g, _, n = scales.shape
    words = np.ascontiguousarray(words).reshape(g, 128, n, -1)
    if fmt == "e4m3":
        vals = words.view(ml_dtypes.float8_e4m3fn).astype(np.float64)
    else:
        nib = np.empty((g, 128, n, 4), np.uint8)
        nib[..., 0::2] = words & 0xF
        nib[..., 1::2] = words >> 4
        vals = E2M1[nib]
    vals = vals * np.repeat(np.exp2(scales.astype(np.float64) - 127.0), 8, axis=1)[..., None]
    return vals.transpose(0, 1, 3, 2).reshape(g * 512, n)


K, T, G, C1, E, C2, H = 512, 1024, 2, 512, 4, 256, 512
N = 128


def by_expert(wq, xq, E, C):
    return np.concatenate([wq[e].T @ xq[:, e * C:(e + 1) * C] for e in range(E)], axis=1)


def setup_inputs():
    n = np.random.standard_normal
    s = mx_kscale(K)
    u = mx_kscale(H)
    slots1 = np.random.permutation(T)
    slots2 = np.concatenate([q * C1 + np.random.permutation(C1) for q in range(G)])
    x = pack_weight(n((K, T)) * s[:, None], "e4m3")
    we = [pack_weight(m, "e2m1") for m in n((E, H, N)) / np.sqrt(H) / u[None, :, None]]
    return {
        "x_words": x[0],
        "x_scales": x[1],
        "wg": (n((G, K, H)) / np.sqrt(K) / s[None, :, None] * u).astype(np.float32),
        "we_words": np.stack([m[0] for m in we]),
        "we_scales": np.stack([m[1] for m in we]),
        "gate": (np.tile(np.random.uniform(0.2, 1.0, T), (128, 1))).astype(np.float32),
        "offs": striped(slots1),
        "offs2": striped(slots2),
        "dst": striped(slots1[slots2]),
    }


def reference(x_words, x_scales, wg, we_words, we_scales, gate, offs, offs2, dst):
    wgq = mxq(f64(wg), 1, "e4m3")
    we = np.stack([unpack_weight(we_words[e], we_scales[e], "e2m1") for e in range(E)])
    idx, idx2 = unstriped(offs), unstriped(offs2)
    xq = unpack_weight(x_words, x_scales, "e4m3")[:, idx]
    a = by_expert(wgq, xq, G, C1)
    y = by_expert(we, mxq(a[:, idx2], 0, "e4m3"), E, C2)
    out = np.zeros((N, T))
    out[:, unstriped(dst)] = f64(gate[:1]) * y
    return out

@@ -1,0 +1,168 @@
+from contextlib import ExitStack
+
+import concourse.mybir as mybir
+
+K, T, G, C1, E, C2, H, N = 512, 1024, 2, 512, 4, 256, 512, 128
+FLOPS = 2 * K * H * T + 2 * H * N * T
+
+F32 = mybir.dt.float32
+BF16 = mybir.dt.bfloat16
+I32 = mybir.dt.int32
+U32 = mybir.dt.uint32
+U16 = mybir.dt.uint16
+U8 = mybir.dt.uint8
+FP8X4 = mybir.dt.float8_e4m3fn_x4
+FP4X4 = mybir.dt.float4_e2m1fn_x4
+COPY = mybir.ActivationFunctionType.Copy
+MULT = mybir.AluOpType.mult
+
+P = 128
+LANES = 16
+
+
+def tile_moe_hie_none_kernel(tc, x_words, x_scales, wg, we_words, we_scales, gate, offs, offs2, dst, out):
+    nc = tc.nc
+    with ExitStack() as ctx:
+        sb = ctx.enter_context(tc.tile_pool(name="sb", bufs=1))
+        pa = ctx.enter_context(tc.psum_pool(name="pa", bufs=6))
+        py = ctx.enter_context(tc.psum_pool(name="py", bufs=2))
+
+        def tile(shape, dtype, name, tag=None):
+            return sb.tile(shape, dtype, name=name, tag=tag or name, align_bytes=64)
+
+        def entries(lst, first, count):
+            return lst[:, first // LANES : (first + count) // LANES]
+
+        offs_t = tile([P, T // LANES], U16, "offs_t")
+        offs2_t = tile([P, T // LANES], U16, "offs2_t")
+        dst_t = tile([P, T // LANES], U16, "dst_t")
+        xw = tile([P, T], I32, "xw")
+        xs = tile([P, T], U8, "xs")
+        raw = [[tile([P, 4, H // 2], F32, "raw%d%d" % (f, h)) for h in range(2)] for f in range(G)]
+        wew = tile([P, E, 2 * N], U8, "wew")
+        wes = tile([P, E, N], U8, "wes")
+        gate_t = tile([P, T], F32, "gate_t")
+        pair00 = tile([P, 2 * C1], BF16, "pair00")
+        pair01 = tile([P, 2 * C1], BF16, "pair01")
+        pair10 = tile([P, 2 * T], BF16, "pair10")
+        planes = tile([P, 3 * C1], BF16, "planes")
+        res = tile([P, T], F32, "res")
+
+        nc.gpsimd.memset(wes[:].rearrange("p e n -> p (e n)").bitcast(I32), 0)
+        nc.gpsimd.memset(pair10[:, 0 : 2 * C1].bitcast(I32), 0)
+        nc.gpsimd.memset(planes[:, 0:C1].bitcast(I32), 0)
+
+        nc.sync.dma_start(offs_t[:], offs)
+        for q in range(4):
+            nc.sync.dma_start(xs[32 * q : 32 * q + 32, :].bitcast(I32), x_scales[0, 4 * q : 4 * q + 4, :].bitcast(I32).unsqueeze(0).broadcast_to([8, 4, T // 4]))
+        nc.sync.dma_start(xw[:], x_words[0].rearrange("p t d -> p (t d)").bitcast(I32))
+        for f, h in ((0, 0), (0, 1), (1, 1), (1, 0)):
+            nc.sync.dma_start(raw[f][h][:], wg[f].rearrange("(p j) c -> p j c", j=4)[:, :, 256 * h : 256 * h + 256])
+        nc.sync.dma_start(offs2_t[:], offs2)
+        nc.sync.dma_start(wew[:].bitcast(I32), we_words[:, 0].rearrange("e p b -> p e b").bitcast(I32))
+        for r in range(4):
+            nc.sync.dma_start(wes[r:P:32].bitcast(I32), we_scales[:, 0, r:16:4, :].rearrange("e q n -> q e n").bitcast(I32))
+        nc.sync.dma_start(dst_t[:], dst)
+        nc.sync.dma_start(gate_t[:], gate)
+
+        xgw = {}
+        xgs = [tile([P, C1], U8, "xgs%d" % f) for f in range(G)]
+
+        def gather_scales(f):
+            nc.vector.tensor_copy(xgs[f][:], xs[:].indirect(entries(offs_t, f * C1, C1)))
+
+        def gather_words(f, tag):
+            xgw[f] = tile([P, C1], U32, "xgw%d" % f, tag)
+            nc.vector.tensor_copy(xgw[f][:], xw[:].bitcast(U32).indirect(entries(offs_t, f * C1, C1)))
+
+        both = tile([P, 8 * H - 256], BF16, "both")
+        grouped = [both[:, 0 : 4 * H], both[:, 4 * H - 256 : 8 * H - 256]]
+        wq = [[tile([P, H // 2], U32, "wq%d%d" % (f, u)) for u in range(2)] for f in range(G)]
+        ws = [[tile([P, H // 2], U8, "ws%d%d" % (f, u)) for u in range(2)] for f in range(G)]
+
+        def cast(f, h, copy):
+            copy(
+                grouped[f].rearrange("p (t m j) -> p m j t", t=4, j=4)[:, 64 * h : 64 * h + 64],
+                raw[f][h][:].rearrange("p j (m t) -> p m j t", t=4),
+            )
+
+        def quantise_wg(f):
+            for u in range(2):
+                nc.vector.quantize_mx(wq[f][u][:].bitcast(FP8X4), ws[f][u][:], grouped[f][:, 1024 * u : 1024 * u + 1024])
+
+        def first_level(f, u, leave):
+            for h in range(2):
+                bank = pa.tile([P, 2, C2], F32, name="bank")
+                cols = slice(C2 * h, C2 * h + C2)
+                for e in range(2):
+                    m = slice(P * e, P * e + P)
+                    nc.tensor.matmul_mx(bank[:, e, :], lhsT=wq[f][u][:, m].bitcast(FP8X4), lhsT_scale=ws[f][u][:, m],
+                                        rhs=xgw[f][:, cols].bitcast(FP8X4), rhs_scale=xgs[f][:, cols], start=True, stop=True)
+                leave(bank, h)
+
+        def into_pairs(pair, first):
+            def leave(bank, h):
+                j0 = first + C2 * h
+                nc.scalar.copy(pair[:].rearrange("p (j e) -> p j e", e=2)[:, j0 : j0 + C2, :], bank[:].rearrange("p e j -> p j e"))
+            return leave
+
+        def into_planes(bank, h):
+            nc.scalar.copy(planes[:, C1:].rearrange("p (e j) -> p e j", e=2)[:, :, C2 * h : C2 * h + C2], bank[:])
+
+        quad = [tile([P, 4 * C2], BF16, "quad%d" % e) for e in range(E)]
+        aq = {}
+        asc = [tile([P, C2], U8, "asc%d" % e) for e in range(E)]
+        ysb = [tile([P, C2], F32, "ysb%d" % e) for e in range(E)]
+
+        def gather_pairs(e, u, pair):
+            nc.vector.tensor_copy(quad[e][:].bitcast(U32).rearrange("p (m u) -> p m u", u=2)[:, :, u],
+                                  pair[:].bitcast(U32).indirect(entries(offs2_t, e * C2, C2)))
+
+        def gather_plane(e, t):
+            first = (t - 2) * C1
+            nc.scalar.activation(quad[e][:].rearrange("p (m t) -> p m t", t=4)[:, :, t],
+                                 planes[:, first : first + T].indirect(entries(offs2_t, e * C2, C2)), COPY)
+
+        def second_level(e, tag=None):
+            aq[e] = tile([P, C2], U32, "aq%d" % e, tag)
+            nc.vector.quantize_mx(aq[e][:].bitcast(FP8X4), asc[e][:], quad[e][:])
+            ybank = py.tile([P, C2], F32, name="ybank")
+            nc.tensor.matmul_mx(ybank[:], lhsT=wew[:, e, :].bitcast(FP4X4), lhsT_scale=wes[:, e, :],
+                                rhs=aq[e][:].bitcast(FP8X4), rhs_scale=asc[e][:], start=True, stop=True)
+            nc.scalar.copy(ysb[e][:], ybank[:])
+
+        def scatter(e):
+            nc.vector.tensor_tensor(res[:].indirect(entries(dst_t, e * C2, C2)), ysb[e][:], gate_t[:, e * C2 : e * C2 + C2], MULT)
+
+        gather_scales(0)
+        gather_words(0, None)
+        gather_scales(1)
+        gather_words(1, None)
+        cast(0, 0, nc.scalar.copy)
+        cast(0, 1, nc.scalar.copy)
+        quantise_wg(0)
+        cast(1, 1, nc.scalar.copy)
+        cast(1, 0, nc.vector.tensor_copy)
+        first_level(0, 0, into_pairs(pair00, 0))
+        first_level(0, 1, into_pairs(pair01, 0))
+        quantise_wg(1)
+        first_level(1, 0, into_pairs(pair10, C1))
+        first_level(1, 1, into_planes)
+        gather_pairs(0, 0, pair00)
+        gather_pairs(1, 0, pair00)
+        gather_pairs(0, 1, pair01)
+        gather_pairs(1, 1, pair01)
+        second_level(0)
+        second_level(1)
+        gather_pairs(2, 0, pair10)
+        gather_pairs(3, 0, pair10)
+        for e in (2, 3):
+            for t in (2, 3):
+                gather_plane(e, t)
+        scatter(0)
+        second_level(2)
+        scatter(1)
+        second_level(3, "ysb0")
+        scatter(2)
+        scatter(3)
+        nc.sync.dma_start(out, res[:])

@@ -13,7 +13,6 @@ U16 = mybir.dt.uint16
 U8 = mybir.dt.uint8
 FP8X4 = mybir.dt.float8_e4m3fn_x4
 FP4X4 = mybir.dt.float4_e2m1fn_x4
-COPY = mybir.ActivationFunctionType.Copy
 MULT = mybir.AluOpType.mult
 
 P = 128
@@ -42,15 +41,15 @@ def tile_moe_hie_none_kernel(tc, x_words, x_scales, wg, we_words, we_scales, gat
         wew = tile([P, E, 2 * N], U8, "wew")
         wes = tile([P, E, N], U8, "wes")
         gate_t = tile([P, T], F32, "gate_t")
-        pair00 = tile([P, 2 * C1], BF16, "pair00")
-        pair01 = tile([P, 2 * C1], BF16, "pair01")
-        pair10 = tile([P, 2 * T], BF16, "pair10")
-        planes = tile([P, 3 * C1], BF16, "planes")
+        SPARE = 256
+        pair = [[tile([P, 2 * (C1 + SPARE)], BF16, "pair00"), tile([P, 2 * C1], BF16, "pair01")],
+                [tile([P, 2 * T], BF16, "pair10"), tile([P, 2 * T], BF16, "pair11")]]
         res = tile([P, T], F32, "res")
 
         nc.gpsimd.memset(wes[:].rearrange("p e n -> p (e n)").bitcast(I32), 0)
-        nc.gpsimd.memset(pair10[:, 0 : 2 * C1].bitcast(I32), 0)
-        nc.gpsimd.memset(planes[:, 0:C1].bitcast(I32), 0)
+        nc.gpsimd.memset(pair[0][0][:, 2 * C1 :].bitcast(I32), 0)
+        for u in range(2):
+            nc.gpsimd.memset(pair[1][u][:, 0 : 2 * C1].bitcast(I32), 0)
 
         nc.sync.dma_start(offs_t[:], offs)
         for q in range(4):
@@ -90,7 +89,7 @@ def tile_moe_hie_none_kernel(tc, x_words, x_scales, wg, we_words, we_scales, gat
             for u in range(2):
                 nc.vector.quantize_mx(wq[f][u][:].bitcast(FP8X4), ws[f][u][:], grouped[f][:, 1024 * u : 1024 * u + 1024])
 
-        def first_level(f, u, leave):
+        def first_level(f, u):
             for h in range(2):
                 bank = pa.tile([P, 2, C2], F32, name="bank")
                 cols = slice(C2 * h, C2 * h + C2)
@@ -98,41 +97,45 @@ def tile_moe_hie_none_kernel(tc, x_words, x_scales, wg, we_words, we_scales, gat
                     m = slice(P * e, P * e + P)
                     nc.tensor.matmul_mx(bank[:, e, :], lhsT=wq[f][u][:, m].bitcast(FP8X4), lhsT_scale=ws[f][u][:, m],
                                         rhs=xgw[f][:, cols].bitcast(FP8X4), rhs_scale=xgs[f][:, cols], start=True, stop=True)
-                leave(bank, h)
+                j0 = f * C1 + C2 * h
+                nc.scalar.copy(pair[f][u][:].rearrange("p (j e) -> p j e", e=2)[:, j0 : j0 + C2, :], bank[:].rearrange("p e j -> p j e"))
 
-        def into_pairs(pair, first):
-            def leave(bank, h):
-                j0 = first + C2 * h
-                nc.scalar.copy(pair[:].rearrange("p (j e) -> p j e", e=2)[:, j0 : j0 + C2, :], bank[:].rearrange("p e j -> p j e"))
-            return leave
+        picked = [tile([P, 2, C1], U32, "picked%d" % f) for f in range(G)]
+        ysb = tile([P, T], F32, "ysb")
+        runs = {"e0": (0, C2), "e1": (C2, C2), "g1": (C1, C1)}
+        quad = {r: tile([P, 4 * runs[r][1]], BF16, "quad" + r) for r in runs}
+        ybank = {}
 
-        def into_planes(bank, h):
-            nc.scalar.copy(planes[:, C1:].rearrange("p (e j) -> p e j", e=2)[:, :, C2 * h : C2 * h + C2], bank[:])
+        def gather_pairs(first, count, u):
+            f, j0 = divmod(first, C1)
+            nc.vector.tensor_copy(picked[f][:, u, j0 : j0 + count], pair[f][u][:].bitcast(U32).indirect(entries(offs2_t, first, count)))
 
-        quad = [tile([P, 4 * C2], BF16, "quad%d" % e) for e in range(E)]
-        aq = {}
-        asc = [tile([P, C2], U8, "asc%d" % e) for e in range(E)]
-        ysb = [tile([P, C2], F32, "ysb%d" % e) for e in range(E)]
+        def weave(r):
+            first, count = runs[r]
+            f, j0 = divmod(first, C1)
+            nc.scalar.copy(quad[r][:].bitcast(U32).rearrange("p (m u) -> p m u", u=2),
+                           picked[f][:, :, j0 : j0 + count].rearrange("p u m -> p m u"))
 
-        def gather_pairs(e, u, pair):
-            nc.vector.tensor_copy(quad[e][:].bitcast(U32).rearrange("p (m u) -> p m u", u=2)[:, :, u],
-                                  pair[:].bitcast(U32).indirect(entries(offs2_t, e * C2, C2)))
+        def second_level(r):
+            first, count = runs[r]
+            aq = tile([P, count], U32, "aq" + r)
+            asc = tile([P, count], U8, "asc" + r)
+            nc.vector.quantize_mx(aq[:].bitcast(FP8X4), asc[:], quad[r][:])
+            ybank[r] = py.tile([P, count], F32, name="ybank")
+            for c0 in range(0, count, C2):
+                e = (first + c0) // C2
+                cols = slice(c0, c0 + C2)
+                nc.tensor.matmul_mx(ybank[r][:, cols], lhsT=wew[:, e, :].bitcast(FP4X4), lhsT_scale=wes[:, e, :],
+                                    rhs=aq[:, cols].bitcast(FP8X4), rhs_scale=asc[:, cols], start=True, stop=True)
 
-        def gather_plane(e, t):
-            first = (t - 2) * C1
-            nc.scalar.activation(quad[e][:].rearrange("p (m t) -> p m t", t=4)[:, :, t],
-                                 planes[:, first : first + T].indirect(entries(offs2_t, e * C2, C2)), COPY)
+        def leave(r):
+            first, count = runs[r]
+            nc.scalar.copy(ysb[:, first : first + count], ybank[r][:])
 
-        def second_level(e, tag=None):
-            aq[e] = tile([P, C2], U32, "aq%d" % e, tag)
-            nc.vector.quantize_mx(aq[e][:].bitcast(FP8X4), asc[e][:], quad[e][:])
-            ybank = py.tile([P, C2], F32, name="ybank")
-            nc.tensor.matmul_mx(ybank[:], lhsT=wew[:, e, :].bitcast(FP4X4), lhsT_scale=wes[:, e, :],
-                                rhs=aq[e][:].bitcast(FP8X4), rhs_scale=asc[e][:], start=True, stop=True)
-            nc.scalar.copy(ysb[e][:], ybank[:])
-
-        def scatter(e):
-            nc.vector.tensor_tensor(res[:].indirect(entries(dst_t, e * C2, C2)), ysb[e][:], gate_t[:, e * C2 : e * C2 + C2], MULT)
+        def scatter(r):
+            first, count = runs[r]
+            cols = slice(first, first + count)
+            nc.vector.tensor_tensor(res[:].indirect(entries(dst_t, first, count)), ysb[:, cols], gate_t[:, cols], MULT)
 
         gather_scales(0)
         gather_words(0, None)
@@ -143,26 +146,26 @@ def tile_moe_hie_none_kernel(tc, x_words, x_scales, wg, we_words, we_scales, gat
         quantise_wg(0)
         cast(1, 1, nc.scalar.copy)
         cast(1, 0, nc.vector.tensor_copy)
-        first_level(0, 0, into_pairs(pair00, 0))
-        first_level(0, 1, into_pairs(pair01, 0))
+        first_level(0, 0)
+        first_level(0, 1)
         quantise_wg(1)
-        first_level(1, 0, into_pairs(pair10, C1))
-        first_level(1, 1, into_planes)
-        gather_pairs(0, 0, pair00)
-        gather_pairs(1, 0, pair00)
-        gather_pairs(0, 1, pair01)
-        gather_pairs(1, 1, pair01)
-        second_level(0)
-        second_level(1)
-        gather_pairs(2, 0, pair10)
-        gather_pairs(3, 0, pair10)
-        for e in (2, 3):
-            for t in (2, 3):
-                gather_plane(e, t)
-        scatter(0)
-        second_level(2)
-        scatter(1)
-        second_level(3, "ysb0")
-        scatter(2)
-        scatter(3)
+        gather_pairs(0, C1, 0)
+        gather_pairs(0, C2, 1)
+        gather_pairs(C2, C2, 1)
+        first_level(1, 0)
+        gather_pairs(C1, C1, 0)
+        weave("e0")
+        second_level("e0")
+        first_level(1, 1)
+        gather_pairs(C1, C1, 1)
+        weave("e1")
+        second_level("e1")
+        leave("e0")
+        scatter("e0")
+        weave("g1")
+        second_level("g1")
+        leave("e1")
+        scatter("e1")
+        leave("g1")
+        scatter("g1")
         nc.sync.dma_start(out, res[:])

@@ -53,7 +53,7 @@ def tile_moe_hie_none_kernel(tc, x_words, x_scales, wg, we_words, we_scales, gat
 
         nc.sync.dma_start(offs_t[:], offs)
         for q in range(4):
-            nc.sync.dma_start(xs[32 * q : 32 * q + 32, :].bitcast(I32), x_scales[0, 4 * q : 4 * q + 4, :].bitcast(I32).unsqueeze(0).broadcast_to([8, 4, T // 4]))
+            (nc.sync if q < 2 else nc.scalar).dma_start(xs[32 * q : 32 * q + 32, :].bitcast(I32), x_scales[0, 4 * q : 4 * q + 4, :].bitcast(I32).unsqueeze(0).broadcast_to([8, 4, T // 4]))
         nc.sync.dma_start(xw[:], x_words[0].rearrange("p t d -> p (t d)").bitcast(I32))
         for f, h in ((0, 0), (0, 1), (1, 1), (1, 0)):
             nc.sync.dma_start(raw[f][h][:], wg[f].rearrange("(p j) c -> p j c", j=4)[:, :, 256 * h : 256 * h + 256])
@@ -70,33 +70,35 @@ def tile_moe_hie_none_kernel(tc, x_words, x_scales, wg, we_words, we_scales, gat
         def gather_scales(f):
             nc.vector.tensor_copy(xgs[f][:], xs[:].indirect(entries(offs_t, f * C1, C1)))
 
-        def gather_words(f, tag):
-            xgw[f] = tile([P, C1], U32, "xgw%d" % f, tag)
-            nc.vector.tensor_copy(xgw[f][:], xw[:].bitcast(U32).indirect(entries(offs_t, f * C1, C1)))
+        def gather_words(f, h, tag=None):
+            count = C1 if f == 0 else C2
+            xgw[f, h] = tile([P, count], U32, "xgw%d%d" % (f, h), tag)
+            nc.vector.tensor_copy(xgw[f, h][:], xw[:].bitcast(U32).indirect(entries(offs_t, f * C1 + h * C2, count)))
 
         both = tile([P, 8 * H - 256], BF16, "both")
         grouped = [both[:, 0 : 4 * H], both[:, 4 * H - 256 : 8 * H - 256]]
-        wq = [[tile([P, H // 2], U32, "wq%d%d" % (f, u)) for u in range(2)] for f in range(G)]
-        ws = [[tile([P, H // 2], U8, "ws%d%d" % (f, u)) for u in range(2)] for f in range(G)]
+        wq = [tile([P, H], U32, "wq%d" % f) for f in range(G)]
+        ws = [tile([P, H], U8, "ws%d" % f) for f in range(G)]
 
-        def cast(f, h, copy):
+        def cast(f, h, copy, t0=0, t1=4):
             copy(
-                grouped[f].rearrange("p (t m j) -> p m j t", t=4, j=4)[:, 64 * h : 64 * h + 64],
-                raw[f][h][:].rearrange("p j (m t) -> p m j t", t=4),
+                grouped[f].rearrange("p (t m j) -> p m j t", t=4, j=4)[:, 64 * h : 64 * h + 64, :, t0:t1],
+                raw[f][h][:].rearrange("p j (m t) -> p m j t", t=4)[:, :, :, t0:t1],
             )
 
-        def quantise_wg(f):
-            for u in range(2):
-                nc.vector.quantize_mx(wq[f][u][:].bitcast(FP8X4), ws[f][u][:], grouped[f][:, 1024 * u : 1024 * u + 1024])
+        def quantise_wg(f, calls):
+            width = H // calls
+            for c0 in range(0, H, width):
+                nc.vector.quantize_mx(wq[f][:, c0 : c0 + width].bitcast(FP8X4), ws[f][:, c0 : c0 + width], grouped[f][:, 4 * c0 : 4 * (c0 + width)])
 
         def first_level(f, u):
             for h in range(2):
                 bank = pa.tile([P, 2, C2], F32, name="bank")
                 cols = slice(C2 * h, C2 * h + C2)
                 for e in range(2):
-                    m = slice(P * e, P * e + P)
-                    nc.tensor.matmul_mx(bank[:, e, :], lhsT=wq[f][u][:, m].bitcast(FP8X4), lhsT_scale=ws[f][u][:, m],
-                                        rhs=xgw[f][:, cols].bitcast(FP8X4), rhs_scale=xgs[f][:, cols], start=True, stop=True)
+                    m = slice(P * (2 * u + e), P * (2 * u + e) + P)
+                    nc.tensor.matmul_mx(bank[:, e, :], lhsT=wq[f][:, m].bitcast(FP8X4), lhsT_scale=ws[f][:, m],
+                                        rhs=(xgw[0, 0][:, cols] if f == 0 else xgw[1, h][:]).bitcast(FP8X4), rhs_scale=xgs[f][:, cols], start=True, stop=True)
                 j0 = f * C1 + C2 * h
                 nc.scalar.copy(pair[f][u][:].rearrange("p (j e) -> p j e", e=2)[:, j0 : j0 + C2, :], bank[:].rearrange("p e j -> p j e"))
 
@@ -138,17 +140,19 @@ def tile_moe_hie_none_kernel(tc, x_words, x_scales, wg, we_words, we_scales, gat
             nc.vector.tensor_tensor(res[:].indirect(entries(dst_t, first, count)), ysb[:, cols], gate_t[:, cols], MULT)
 
         gather_scales(0)
-        gather_words(0, None)
+        gather_words(0, 0)
         gather_scales(1)
-        gather_words(1, None)
+        gather_words(1, 0)
         cast(0, 0, nc.scalar.copy)
-        cast(0, 1, nc.scalar.copy)
-        quantise_wg(0)
+        cast(0, 1, nc.scalar.copy, 0, 2)
+        cast(0, 1, nc.scalar.copy, 2, 4)
+        quantise_wg(0, 2)
+        gather_words(1, 1, "raw01")
         cast(1, 1, nc.scalar.copy)
         cast(1, 0, nc.vector.tensor_copy)
         first_level(0, 0)
         first_level(0, 1)
-        quantise_wg(1)
+        quantise_wg(1, 1)
         gather_pairs(0, C1, 0)
         gather_pairs(0, C2, 1)
         gather_pairs(C2, C2, 1)

@@ -16,160 +16,190 @@ FP4X4 = mybir.dt.float4_e2m1fn_x4
 MULT = mybir.AluOpType.mult
 
 P = 128
-LANES = 16
+PACK = 4
+QUADRANT = 32
+PER_COLUMN = 16
+HALF = H // 2
+SPARE = 256
+SHARED = 256
+A_BANKS, Y_BANKS = 6, 2
 
 
 def tile_moe_hie_none_kernel(tc, x_words, x_scales, wg, we_words, we_scales, gate, offs, offs2, dst, out):
     nc = tc.nc
     with ExitStack() as ctx:
-        sb = ctx.enter_context(tc.tile_pool(name="sb", bufs=1))
-        pa = ctx.enter_context(tc.psum_pool(name="pa", bufs=6))
-        py = ctx.enter_context(tc.psum_pool(name="py", bufs=2))
+        sbuf = ctx.enter_context(tc.tile_pool(name="sbuf", bufs=1))
+        a_psum = ctx.enter_context(tc.psum_pool(name="a_psum", bufs=A_BANKS))
+        y_psum = ctx.enter_context(tc.psum_pool(name="y_psum", bufs=Y_BANKS))
 
         def tile(shape, dtype, name, tag=None):
-            return sb.tile(shape, dtype, name=name, tag=tag or name, align_bytes=64)
+            return sbuf.tile(shape, dtype, name=name, tag=tag or name, align_bytes=64)
 
-        def entries(lst, first, count):
-            return lst[:, first // LANES : (first + count) // LANES]
+        def entries(list_tile, first, count):
+            return list_tile[:, first // PER_COLUMN : (first + count) // PER_COLUMN]
 
-        offs_t = tile([P, T // LANES], U16, "offs_t")
-        offs2_t = tile([P, T // LANES], U16, "offs2_t")
-        dst_t = tile([P, T // LANES], U16, "dst_t")
-        xw = tile([P, T], I32, "xw")
-        xs = tile([P, T], U8, "xs")
-        raw = [[tile([P, 4, H // 2], F32, "raw%d%d" % (f, h)) for h in range(2)] for f in range(G)]
-        wew = tile([P, E, 2 * N], U8, "wew")
-        wes = tile([P, E, N], U8, "wes")
+        offs_t = tile([P, T // PER_COLUMN], U16, "offs_t")
+        offs2_t = tile([P, T // PER_COLUMN], U16, "offs2_t")
+        dst_t = tile([P, T // PER_COLUMN], U16, "dst_t")
+        token_words = tile([P, T], I32, "token_words")
+        token_scales = tile([P, T], U8, "token_scales")
+        wg_raw = [[tile([P, PACK, HALF], F32, "wg_raw%d%d" % (f, h)) for h in range(2)] for f in range(G)]
+        we_w = tile([P, E, 2 * N], U8, "we_w")
+        we_s = tile([P, E, N], U8, "we_s")
         gate_t = tile([P, T], F32, "gate_t")
-        SPARE = 256
-        pair = [[tile([P, 2 * (C1 + SPARE)], BF16, "pair00"), tile([P, 2 * C1], BF16, "pair01")],
-                [tile([P, 2 * T], BF16, "pair10"), tile([P, 2 * T], BF16, "pair11")]]
-        res = tile([P, T], F32, "res")
+        pairs = [
+            [tile([P, 2 * (C1 + SPARE)], BF16, "pairs00"), tile([P, 2 * C1], BF16, "pairs01")],
+            [tile([P, 2 * T], BF16, "pairs10"), tile([P, 2 * T], BF16, "pairs11")],
+        ]
+        result = tile([P, T], F32, "result")
 
-        nc.gpsimd.memset(wes[:].rearrange("p e n -> p (e n)").bitcast(I32), 0)
-        nc.gpsimd.memset(pair[0][0][:, 2 * C1 :].bitcast(I32), 0)
+        nc.vector.memset(we_s[:].rearrange("p e n -> p (e n)").bitcast(I32), 0)
+        nc.vector.memset(pairs[0][0][:, 2 * C1 :].bitcast(I32), 0)
         for u in range(2):
-            nc.gpsimd.memset(pair[1][u][:, 0 : 2 * C1].bitcast(I32), 0)
+            nc.vector.memset(pairs[1][u][:, 0 : 2 * C1].bitcast(I32), 0)
 
         nc.sync.dma_start(offs_t[:], offs)
-        for q in range(4):
-            (nc.sync if q < 2 else nc.scalar).dma_start(xs[32 * q : 32 * q + 32, :].bitcast(I32), x_scales[0, 4 * q : 4 * q + 4, :].bitcast(I32).unsqueeze(0).broadcast_to([8, 4, T // 4]))
-        nc.sync.dma_start(xw[:], x_words[0].rearrange("p t d -> p (t d)").bitcast(I32))
+        for q in range(P // QUADRANT):
+            queue = nc.sync if q < 2 else nc.scalar
+            rows = x_scales[0, 4 * q : 4 * q + 4, :].bitcast(I32)
+            queue.dma_start(
+                token_scales[QUADRANT * q : QUADRANT * (q + 1), :].bitcast(I32),
+                rows.unsqueeze(0).broadcast_to([QUADRANT // 4, 4, T // 4]),
+            )
+        nc.sync.dma_start(token_words[:], x_words[0].rearrange("p t d -> p (t d)").bitcast(I32))
         for f, h in ((0, 0), (0, 1), (1, 1), (1, 0)):
-            nc.sync.dma_start(raw[f][h][:], wg[f].rearrange("(p j) c -> p j c", j=4)[:, :, 256 * h : 256 * h + 256])
+            nc.sync.dma_start(wg_raw[f][h][:], wg[f].rearrange("(p j) c -> p j c", j=PACK)[:, :, HALF * h : HALF * (h + 1)])
         nc.sync.dma_start(offs2_t[:], offs2)
-        nc.sync.dma_start(wew[:].bitcast(I32), we_words[:, 0].rearrange("e p b -> p e b").bitcast(I32))
+        nc.sync.dma_start(we_w[:].bitcast(I32), we_words[:, 0].rearrange("e p b -> p e b").bitcast(I32))
         for r in range(4):
-            nc.sync.dma_start(wes[r:P:32].bitcast(I32), we_scales[:, 0, r:16:4, :].rearrange("e q n -> q e n").bitcast(I32))
+            nc.sync.dma_start(we_s[r:P:QUADRANT].bitcast(I32), we_scales[:, 0, r:16:4, :].rearrange("e q n -> q e n").bitcast(I32))
         nc.sync.dma_start(dst_t[:], dst)
         nc.sync.dma_start(gate_t[:], gate)
 
-        xgw = {}
-        xgs = [tile([P, C1], U8, "xgs%d" % f) for f in range(G)]
+        slot_words = {}
+        slot_scales = [tile([P, C1], U8, "slot_scales%d" % f) for f in range(G)]
 
         def gather_scales(f):
-            nc.vector.tensor_copy(xgs[f][:], xs[:].indirect(entries(offs_t, f * C1, C1)))
+            nc.vector.tensor_copy(slot_scales[f][:], token_scales[:].indirect(entries(offs_t, f * C1, C1)))
 
-        def gather_words(f, h, tag=None):
-            count = C1 if f == 0 else C2
-            xgw[f, h] = tile([P, count], U32, "xgw%d%d" % (f, h), tag)
-            nc.vector.tensor_copy(xgw[f, h][:], xw[:].bitcast(U32).indirect(entries(offs_t, f * C1 + h * C2, count)))
+        def gather_words(first, count, tag=None):
+            slot_words[first] = tile([P, count], U32, "slot_words%d" % first, tag)
+            nc.vector.tensor_copy(slot_words[first][:], token_words[:].bitcast(U32).indirect(entries(offs_t, first, count)))
 
-        both = tile([P, 8 * H - 256], BF16, "both")
-        grouped = [both[:, 0 : 4 * H], both[:, 4 * H - 256 : 8 * H - 256]]
-        wq = [tile([P, H], U32, "wq%d" % f) for f in range(G)]
-        ws = [tile([P, H], U8, "ws%d" % f) for f in range(G)]
+        def words_of(first):
+            start = max(s for s in slot_words if s <= first)
+            return slot_words[start][:, first - start : first - start + C2]
 
-        def cast(f, h, copy, t0=0, t1=4):
+        wg_both = tile([P, 2 * PACK * H - SHARED], BF16, "wg_both")
+        wg_bf = [wg_both[:, 0 : PACK * H], wg_both[:, PACK * H - SHARED : 2 * PACK * H - SHARED]]
+        wg_codes = [tile([P, H], U32, "wg_codes%d" % f) for f in range(G)]
+        wg_scales = [tile([P, H], U8, "wg_scales%d" % f) for f in range(G)]
+
+        def round_wg(f, h, copy, t0=0, t1=PACK):
+            m0, m1 = h * HALF // PACK, (h + 1) * HALF // PACK
             copy(
-                grouped[f].rearrange("p (t m j) -> p m j t", t=4, j=4)[:, 64 * h : 64 * h + 64, :, t0:t1],
-                raw[f][h][:].rearrange("p j (m t) -> p m j t", t=4)[:, :, :, t0:t1],
+                wg_bf[f].rearrange("p (t m j) -> p m j t", t=PACK, j=PACK)[:, m0:m1, :, t0:t1],
+                wg_raw[f][h][:].rearrange("p j (m t) -> p m j t", t=PACK)[:, :, :, t0:t1],
             )
 
         def quantise_wg(f, calls):
             width = H // calls
             for c0 in range(0, H, width):
-                nc.vector.quantize_mx(wq[f][:, c0 : c0 + width].bitcast(FP8X4), ws[f][:, c0 : c0 + width], grouped[f][:, 4 * c0 : 4 * (c0 + width)])
+                cols = slice(c0, c0 + width)
+                nc.vector.quantize_mx(wg_codes[f][:, cols].bitcast(FP8X4), wg_scales[f][:, cols], wg_bf[f][:, PACK * c0 : PACK * (c0 + width)])
 
         def first_level(f, u):
-            for h in range(2):
-                bank = pa.tile([P, 2, C2], F32, name="bank")
-                cols = slice(C2 * h, C2 * h + C2)
-                for e in range(2):
-                    m = slice(P * (2 * u + e), P * (2 * u + e) + P)
-                    nc.tensor.matmul_mx(bank[:, e, :], lhsT=wq[f][:, m].bitcast(FP8X4), lhsT_scale=ws[f][:, m],
-                                        rhs=(xgw[0, 0][:, cols] if f == 0 else xgw[1, h][:]).bitcast(FP8X4), rhs_scale=xgs[f][:, cols], start=True, stop=True)
-                j0 = f * C1 + C2 * h
-                nc.scalar.copy(pair[f][u][:].rearrange("p (j e) -> p j e", e=2)[:, j0 : j0 + C2, :], bank[:].rearrange("p e j -> p j e"))
+            for c0 in range(0, C1, C2):
+                bank = a_psum.tile([P, 2, C2], F32, name="a_bank")
+                first = f * C1 + c0
+                for d in range(2):
+                    places = slice(P * (2 * u + d), P * (2 * u + d + 1))
+                    nc.tensor.matmul_mx(
+                        bank[:, d, :],
+                        lhsT=wg_codes[f][:, places].bitcast(FP8X4),
+                        lhsT_scale=wg_scales[f][:, places],
+                        rhs=words_of(first).bitcast(FP8X4),
+                        rhs_scale=slot_scales[f][:, c0 : c0 + C2],
+                        start=True,
+                        stop=True,
+                    )
+                nc.scalar.copy(
+                    pairs[f][u][:].rearrange("p (s d) -> p s d", d=2)[:, first : first + C2, :],
+                    bank[:].rearrange("p d s -> p s d"),
+                )
 
         picked = [tile([P, 2, C1], U32, "picked%d" % f) for f in range(G)]
-        ysb = tile([P, T], F32, "ysb")
-        runs = {"e0": (0, C2), "e1": (C2, C2), "g1": (C1, C1)}
-        quad = {r: tile([P, 4 * runs[r][1]], BF16, "quad" + r) for r in runs}
-        ybank = {}
+        y = tile([P, T], F32, "y")
+        expert0, expert1, group1 = (0, C2), (C2, C2), (C1, C1)
+        a_bf = {run: tile([P, PACK * run[1]], BF16, "a_bf%d" % run[0]) for run in (expert0, expert1, group1)}
+        y_banks = {}
 
-        def gather_pairs(first, count, u):
-            f, j0 = divmod(first, C1)
-            nc.vector.tensor_copy(picked[f][:, u, j0 : j0 + count], pair[f][u][:].bitcast(U32).indirect(entries(offs2_t, first, count)))
+        def gather_pairs(run, u):
+            first, count = run
+            f, s0 = divmod(first, C1)
+            nc.vector.tensor_copy(picked[f][:, u, s0 : s0 + count], pairs[f][u][:].bitcast(U32).indirect(entries(offs2_t, first, count)))
 
-        def weave(r):
-            first, count = runs[r]
-            f, j0 = divmod(first, C1)
-            nc.scalar.copy(quad[r][:].bitcast(U32).rearrange("p (m u) -> p m u", u=2),
-                           picked[f][:, :, j0 : j0 + count].rearrange("p u m -> p m u"))
+        def join_pairs(run):
+            first, count = run
+            f, s0 = divmod(first, C1)
+            nc.scalar.copy(
+                a_bf[run][:].bitcast(U32).rearrange("p (s u) -> p s u", u=2),
+                picked[f][:, :, s0 : s0 + count].rearrange("p u s -> p s u"),
+            )
 
-        def second_level(r):
-            first, count = runs[r]
-            aq = tile([P, count], U32, "aq" + r)
-            asc = tile([P, count], U8, "asc" + r)
-            nc.vector.quantize_mx(aq[:].bitcast(FP8X4), asc[:], quad[r][:])
-            ybank[r] = py.tile([P, count], F32, name="ybank")
+        def second_level(run):
+            first, count = run
+            a_codes = tile([P, count], U32, "a_codes%d" % first)
+            a_scales = tile([P, count], U8, "a_scales%d" % first)
+            nc.vector.quantize_mx(a_codes[:].bitcast(FP8X4), a_scales[:], a_bf[run][:])
+            y_banks[run] = y_psum.tile([P, count], F32, name="y_bank")
             for c0 in range(0, count, C2):
                 e = (first + c0) // C2
                 cols = slice(c0, c0 + C2)
-                nc.tensor.matmul_mx(ybank[r][:, cols], lhsT=wew[:, e, :].bitcast(FP4X4), lhsT_scale=wes[:, e, :],
-                                    rhs=aq[:, cols].bitcast(FP8X4), rhs_scale=asc[:, cols], start=True, stop=True)
+                nc.tensor.matmul_mx(
+                    y_banks[run][:, cols],
+                    lhsT=we_w[:, e, :].bitcast(FP4X4),
+                    lhsT_scale=we_s[:, e, :],
+                    rhs=a_codes[:, cols].bitcast(FP8X4),
+                    rhs_scale=a_scales[:, cols],
+                    start=True,
+                    stop=True,
+                )
 
-        def leave(r):
-            first, count = runs[r]
-            nc.scalar.copy(ysb[:, first : first + count], ybank[r][:])
-
-        def scatter(r):
-            first, count = runs[r]
+        def scatter(run):
+            first, count = run
             cols = slice(first, first + count)
-            nc.vector.tensor_tensor(res[:].indirect(entries(dst_t, first, count)), ysb[:, cols], gate_t[:, cols], MULT)
+            nc.scalar.copy(y[:, cols], y_banks[run][:])
+            nc.vector.tensor_tensor(result[:].indirect(entries(dst_t, first, count)), y[:, cols], gate_t[:, cols], MULT)
 
         gather_scales(0)
-        gather_words(0, 0)
+        gather_words(0, C1)
         gather_scales(1)
-        gather_words(1, 0)
-        cast(0, 0, nc.scalar.copy)
-        cast(0, 1, nc.scalar.copy, 0, 2)
-        cast(0, 1, nc.scalar.copy, 2, 4)
+        gather_words(C1, C2)
+        round_wg(0, 0, nc.scalar.copy)
+        round_wg(0, 1, nc.scalar.copy, 0, 2)
+        round_wg(0, 1, nc.scalar.copy, 2, PACK)
         quantise_wg(0, 2)
-        gather_words(1, 1, "raw01")
-        cast(1, 1, nc.scalar.copy)
-        cast(1, 0, nc.vector.tensor_copy)
+        gather_words(C1 + C2, C2, "wg_raw01")
+        round_wg(1, 1, nc.scalar.copy)
+        round_wg(1, 0, nc.vector.tensor_copy)
         first_level(0, 0)
         first_level(0, 1)
         quantise_wg(1, 1)
-        gather_pairs(0, C1, 0)
-        gather_pairs(0, C2, 1)
-        gather_pairs(C2, C2, 1)
+        gather_pairs((0, C1), 0)
+        gather_pairs(expert0, 1)
+        gather_pairs(expert1, 1)
         first_level(1, 0)
-        gather_pairs(C1, C1, 0)
-        weave("e0")
-        second_level("e0")
+        gather_pairs(group1, 0)
+        join_pairs(expert0)
+        second_level(expert0)
         first_level(1, 1)
-        gather_pairs(C1, C1, 1)
-        weave("e1")
-        second_level("e1")
-        leave("e0")
-        scatter("e0")
-        weave("g1")
-        second_level("g1")
-        leave("e1")
-        scatter("e1")
-        leave("g1")
-        scatter("g1")
-        nc.sync.dma_start(out, res[:])
+        gather_pairs(group1, 1)
+        join_pairs(expert1)
+        second_level(expert1)
+        scatter(expert0)
+        join_pairs(group1)
+        second_level(group1)
+        scatter(expert1)
+        scatter(group1)
+        nc.sync.dma_start(out, result[:])

@@ -14,6 +14,7 @@ U8 = mybir.dt.uint8
 FP8X4 = mybir.dt.float8_e4m3fn_x4
 FP4X4 = mybir.dt.float4_e2m1fn_x4
 MULT = mybir.AluOpType.mult
+COPY = mybir.ActivationFunctionType.Copy
 
 P = 128
 PACK = 4
@@ -49,14 +50,15 @@ def tile_moe_hie_none_kernel(tc, x_words, x_scales, wg, we_words, we_scales, gat
         gate_t = tile([P, T], F32, "gate_t")
         pairs = [
             [tile([P, 2 * (C1 + SPARE)], BF16, "pairs00"), tile([P, 2 * C1], BF16, "pairs01")],
-            [tile([P, 2 * T], BF16, "pairs10"), tile([P, 2 * T], BF16, "pairs11")],
+            [tile([P, 2 * T], BF16, "pairs10")],
         ]
+        planes = tile([P, 3 * C1], BF16, "planes")
         result = tile([P, T], F32, "result")
 
         nc.vector.memset(we_s[:].rearrange("p e n -> p (e n)").bitcast(I32), 0)
         nc.vector.memset(pairs[0][0][:, 2 * C1 :].bitcast(I32), 0)
-        for u in range(2):
-            nc.vector.memset(pairs[1][u][:, 0 : 2 * C1].bitcast(I32), 0)
+        nc.vector.memset(pairs[1][0][:, 0 : 2 * C1].bitcast(I32), 0)
+        nc.vector.memset(planes[:, 0:C1].bitcast(I32), 0)
 
         nc.sync.dma_start(offs_t[:], offs)
         for q in range(P // QUADRANT):
@@ -66,9 +68,14 @@ def tile_moe_hie_none_kernel(tc, x_words, x_scales, wg, we_words, we_scales, gat
                 token_scales[QUADRANT * q : QUADRANT * (q + 1), :].bitcast(I32),
                 rows.unsqueeze(0).broadcast_to([QUADRANT // 4, 4, T // 4]),
             )
-        nc.sync.dma_start(token_words[:], x_words[0].rearrange("p t d -> p (t d)").bitcast(I32))
-        for f, h in ((0, 0), (0, 1), (1, 1), (1, 0)):
+
+        def load_wg(f, h):
             nc.sync.dma_start(wg_raw[f][h][:], wg[f].rearrange("(p j) c -> p j c", j=PACK)[:, :, HALF * h : HALF * (h + 1)])
+
+        load_wg(0, 0)
+        nc.sync.dma_start(token_words[:], x_words[0].rearrange("p t d -> p (t d)").bitcast(I32))
+        for f, h in ((0, 1), (1, 0), (1, 1)):
+            load_wg(f, h)
         nc.sync.dma_start(offs2_t[:], offs2)
         nc.sync.dma_start(we_w[:].bitcast(I32), we_words[:, 0].rearrange("e p b -> p e b").bitcast(I32))
         for r in range(4):
@@ -90,116 +97,147 @@ def tile_moe_hie_none_kernel(tc, x_words, x_scales, wg, we_words, we_scales, gat
             start = max(s for s in slot_words if s <= first)
             return slot_words[start][:, first - start : first - start + C2]
 
-        wg_both = tile([P, 2 * PACK * H - SHARED], BF16, "wg_both")
-        wg_bf = [wg_both[:, 0 : PACK * H], wg_both[:, PACK * H - SHARED : 2 * PACK * H - SHARED]]
+        wg_first = tile([P, 2 * H], BF16, "wg_first")
+        wg_rest = tile([P, 2304], BF16, "wg_rest")
+        wg_bf = [[wg_first[:], wg_rest[:, 768:1792]], [wg_rest[:, 1280:2304], wg_rest[:, 0:1024]]]
         wg_codes = [tile([P, H], U32, "wg_codes%d" % f) for f in range(G)]
         wg_scales = [tile([P, H], U8, "wg_scales%d" % f) for f in range(G)]
 
-        def round_wg(f, h, copy, t0=0, t1=PACK):
+        def round_wg(f, h, u, copy):
             m0, m1 = h * HALF // PACK, (h + 1) * HALF // PACK
             copy(
-                wg_bf[f].rearrange("p (t m j) -> p m j t", t=PACK, j=PACK)[:, m0:m1, :, t0:t1],
-                wg_raw[f][h][:].rearrange("p j (m t) -> p m j t", t=PACK)[:, :, :, t0:t1],
+                wg_bf[f][u].rearrange("p (t m j) -> p m j t", t=2, j=PACK)[:, m0:m1],
+                wg_raw[f][h][:].rearrange("p j (m t) -> p m j t", t=PACK)[:, :, :, 2 * u : 2 * u + 2],
             )
 
-        def quantise_wg(f, calls):
-            width = H // calls
-            for c0 in range(0, H, width):
-                cols = slice(c0, c0 + width)
-                nc.vector.quantize_mx(wg_codes[f][:, cols].bitcast(FP8X4), wg_scales[f][:, cols], wg_bf[f][:, PACK * c0 : PACK * (c0 + width)])
+        def quantise_wg(f):
+            for u in range(2):
+                cols = slice(u * HALF, (u + 1) * HALF)
+                nc.vector.quantize_mx(wg_codes[f][:, cols].bitcast(FP8X4), wg_scales[f][:, cols], wg_bf[f][u])
 
-        def first_level(f, u):
-            for c0 in range(0, C1, C2):
-                bank = a_psum.tile([P, 2, C2], F32, name="a_bank")
-                first = f * C1 + c0
-                for d in range(2):
-                    places = slice(P * (2 * u + d), P * (2 * u + d + 1))
-                    nc.tensor.matmul_mx(
-                        bank[:, d, :],
-                        lhsT=wg_codes[f][:, places].bitcast(FP8X4),
-                        lhsT_scale=wg_scales[f][:, places],
-                        rhs=words_of(first).bitcast(FP8X4),
-                        rhs_scale=slot_scales[f][:, c0 : c0 + C2],
-                        start=True,
-                        stop=True,
-                    )
-                nc.scalar.copy(
-                    pairs[f][u][:].rearrange("p (s d) -> p s d", d=2)[:, first : first + C2, :],
-                    bank[:].rearrange("p d s -> p s d"),
-                )
-
-        picked = [tile([P, 2, C1], U32, "picked%d" % f) for f in range(G)]
-        y = tile([P, T], F32, "y")
-        expert0, expert1, group1 = (0, C2), (C2, C2), (C1, C1)
-        a_bf = {run: tile([P, PACK * run[1]], BF16, "a_bf%d" % run[0]) for run in (expert0, expert1, group1)}
-        y_banks = {}
-
-        def gather_pairs(run, u):
-            first, count = run
-            f, s0 = divmod(first, C1)
-            nc.vector.tensor_copy(picked[f][:, u, s0 : s0 + count], pairs[f][u][:].bitcast(U32).indirect(entries(offs2_t, first, count)))
-
-        def join_pairs(run):
-            first, count = run
-            f, s0 = divmod(first, C1)
-            nc.scalar.copy(
-                a_bf[run][:].bitcast(U32).rearrange("p (s u) -> p s u", u=2),
-                picked[f][:, :, s0 : s0 + count].rearrange("p u s -> p s u"),
-            )
-
-        def second_level(run):
-            first, count = run
-            a_codes = tile([P, count], U32, "a_codes%d" % first)
-            a_scales = tile([P, count], U8, "a_scales%d" % first)
-            nc.vector.quantize_mx(a_codes[:].bitcast(FP8X4), a_scales[:], a_bf[run][:])
-            y_banks[run] = y_psum.tile([P, count], F32, name="y_bank")
-            for c0 in range(0, count, C2):
-                e = (first + c0) // C2
-                cols = slice(c0, c0 + C2)
+        def first_level(f, u, c0):
+            bank = a_psum.tile([P, 2, C2], F32, name="a_bank")
+            first = f * C1 + c0
+            for d in range(2):
+                places = slice(P * (2 * u + d), P * (2 * u + d + 1))
                 nc.tensor.matmul_mx(
-                    y_banks[run][:, cols],
-                    lhsT=we_w[:, e, :].bitcast(FP4X4),
-                    lhsT_scale=we_s[:, e, :],
-                    rhs=a_codes[:, cols].bitcast(FP8X4),
-                    rhs_scale=a_scales[:, cols],
+                    bank[:, d, :],
+                    lhsT=wg_codes[f][:, places].bitcast(FP8X4),
+                    lhsT_scale=wg_scales[f][:, places],
+                    rhs=words_of(first).bitcast(FP8X4),
+                    rhs_scale=slot_scales[f][:, c0 : c0 + C2],
                     start=True,
                     stop=True,
                 )
+            nc.scalar.copy(
+                pairs[f][u][:].rearrange("p (s d) -> p s d", d=2)[:, first : first + C2, :],
+                bank[:].rearrange("p d s -> p s d"),
+            )
 
-        def scatter(run):
-            first, count = run
-            cols = slice(first, first + count)
-            nc.scalar.copy(y[:, cols], y_banks[run][:])
-            nc.vector.tensor_tensor(result[:].indirect(entries(dst_t, first, count)), y[:, cols], gate_t[:, cols], MULT)
+        def first_level_plane(d):
+            bank = a_psum.tile([P, C1], F32, name="a_bank")
+            places = slice(P * (2 + d), P * (3 + d))
+            for c0 in (0, C2):
+                nc.tensor.matmul_mx(
+                    bank[:, c0 : c0 + C2],
+                    lhsT=wg_codes[1][:, places].bitcast(FP8X4),
+                    lhsT_scale=wg_scales[1][:, places],
+                    rhs=words_of(C1 + c0).bitcast(FP8X4),
+                    rhs_scale=slot_scales[1][:, c0 : c0 + C2],
+                    start=True,
+                    stop=True,
+                )
+            nc.scalar.copy(planes[:, (1 + d) * C1 : (2 + d) * C1], bank[:])
+
+        picked = {}
+        a_bf = {}
+        y_banks = {}
+
+        def gather_pairs(target, first, count, u):
+            f = first // C1
+            nc.vector.tensor_copy(target, pairs[f][u][:].bitcast(U32).indirect(entries(offs2_t, first, count)))
+
+        def gather_plane(e, d):
+            nc.scalar.activation(
+                picked[e][:, 1, :].bitcast(BF16).rearrange("p (s d) -> p s d", d=2)[:, :, d],
+                planes[:, d * C1 : d * C1 + T].indirect(entries(offs2_t, e * C2, C2)),
+                COPY,
+            )
+
+        def join_pairs(e):
+            a_bf[e] = tile([P, PACK * C2], BF16, "a_bf%d" % e)
+            nc.scalar.copy(
+                a_bf[e][:].bitcast(U32).rearrange("p (s u) -> p s u", u=2),
+                picked[e].rearrange("p u s -> p s u"),
+            )
+
+        def second_level(e):
+            a_codes = tile([P, C2], U32, "a_codes%d" % e)
+            a_scales = tile([P, C2], U8, "a_scales%d" % e)
+            nc.vector.quantize_mx(a_codes[:].bitcast(FP8X4), a_scales[:], a_bf[e][:])
+            y_banks[e] = y_psum.tile([P, C2], F32, name="y_bank")
+            nc.tensor.matmul_mx(
+                y_banks[e][:],
+                lhsT=we_w[:, e, :].bitcast(FP4X4),
+                lhsT_scale=we_s[:, e, :],
+                rhs=a_codes[:].bitcast(FP8X4),
+                rhs_scale=a_scales[:],
+                start=True,
+                stop=True,
+            )
+
+        def scatter(first, count, copy):
+            e, c0 = divmod(first, C2)
+            y = tile([P, count], F32, "y%d" % first)
+            copy(y[:], y_banks[e][:, c0 : c0 + count])
+            nc.vector.tensor_tensor(result[:].indirect(entries(dst_t, first, count)), y[:], gate_t[:, first : first + count], MULT)
 
         gather_scales(0)
-        gather_words(0, C1)
         gather_scales(1)
+        gather_words(0, C1)
         gather_words(C1, C2)
-        round_wg(0, 0, nc.scalar.copy)
-        round_wg(0, 1, nc.scalar.copy, 0, 2)
-        round_wg(0, 1, nc.scalar.copy, 2, PACK)
-        quantise_wg(0, 2)
+        for h in range(2):
+            for u in range(2):
+                round_wg(0, h, u, nc.scalar.copy)
+        quantise_wg(0)
         gather_words(C1 + C2, C2, "wg_raw01")
-        round_wg(1, 1, nc.scalar.copy)
-        round_wg(1, 0, nc.vector.tensor_copy)
-        first_level(0, 0)
-        first_level(0, 1)
-        quantise_wg(1, 1)
-        gather_pairs((0, C1), 0)
-        gather_pairs(expert0, 1)
-        gather_pairs(expert1, 1)
-        first_level(1, 0)
-        gather_pairs(group1, 0)
-        join_pairs(expert0)
-        second_level(expert0)
-        first_level(1, 1)
-        gather_pairs(group1, 1)
-        join_pairs(expert1)
-        second_level(expert1)
-        scatter(expert0)
-        join_pairs(group1)
-        second_level(group1)
-        scatter(expert1)
-        scatter(group1)
+        round_wg(1, 0, 1, nc.scalar.copy)
+        round_wg(1, 0, 0, nc.vector.tensor_copy)
+        round_wg(1, 1, 0, nc.vector.tensor_copy)
+        round_wg(1, 1, 1, nc.vector.tensor_copy)
+        for u in range(2):
+            for c0 in (0, C2):
+                first_level(0, u, c0)
+        quantise_wg(1)
+        picked0 = tile([P, 2, C1], U32, "picked0")
+        picked[0], picked[1] = picked0[:, :, 0:C2], picked0[:, :, C2:C1]
+        gather_pairs(picked0[:, 0, :], 0, C1, 0)
+        gather_pairs(picked[0][:, 1, :], 0, C2, 1)
+        gather_pairs(picked[1][:, 1, :], C2, C2, 1)
+        first_level(1, 0, 0)
+        first_level(1, 0, C2)
+        picked2 = tile([P, 2, C2], U32, "picked2")
+        picked[2] = picked2[:]
+        gather_pairs(picked[2][:, 0, :], 2 * C2, C2, 0)
+        first_level_plane(0)
+        join_pairs(0)
+        second_level(0)
+        picked3 = tile([P, 2, C2], U32, "picked3", "a_bf0")
+        picked[3] = picked3[:]
+        gather_pairs(picked[3][:, 0, :], 3 * C2, C2, 0)
+        first_level_plane(1)
+        join_pairs(1)
+        second_level(1)
+        scatter(0, C2, nc.vector.tensor_copy)
+        gather_plane(2, 0)
+        gather_plane(2, 1)
+        gather_plane(3, 0)
+        join_pairs(2)
+        second_level(2)
+        scatter(C2, C2, nc.scalar.copy)
+        gather_plane(3, 1)
+        join_pairs(3)
+        second_level(3)
+        scatter(2 * C2, C2, nc.scalar.copy)
+        scatter(3 * C2, C2, nc.scalar.copy)
         nc.sync.dma_start(out, result[:])

@@ -21,6 +21,7 @@ PACK = 4
 QUADRANT = 32
 PER_COLUMN = 16
 HALF = H // 2
+SCALE_SPARE = 384
 SPARE = 256
 SHARED = 256
 A_BANKS, Y_BANKS = 6, 2
@@ -43,7 +44,7 @@ def tile_moe_hie_none_kernel(tc, x_words, x_scales, wg, we_words, we_scales, gat
         offs2_t = tile([P, T // PER_COLUMN], U16, "offs2_t")
         dst_t = tile([P, T // PER_COLUMN], U16, "dst_t")
         token_words = tile([P, T], I32, "token_words")
-        token_scales = tile([P, T], U8, "token_scales")
+        token_scales = tile([P, T + SCALE_SPARE], U8, "token_scales")
         wg_raw = [[tile([P, PACK, HALF], F32, "wg_raw%d%d" % (f, h)) for h in range(2)] for f in range(G)]
         we_w = tile([P, E, 2 * N], U8, "we_w")
         we_s = tile([P, E, N], U8, "we_s")
@@ -56,6 +57,7 @@ def tile_moe_hie_none_kernel(tc, x_words, x_scales, wg, we_words, we_scales, gat
         result = tile([P, T], F32, "result")
 
         nc.vector.memset(we_s[:].rearrange("p e n -> p (e n)").bitcast(I32), 0)
+        nc.vector.memset(token_scales[:, T:].bitcast(I32), 0)
         nc.vector.memset(pairs[0][0][:, 2 * C1 :].bitcast(I32), 0)
         nc.vector.memset(pairs[1][0][:, 0 : 2 * C1].bitcast(I32), 0)
         nc.vector.memset(planes[:, 0:C1].bitcast(I32), 0)
@@ -65,7 +67,7 @@ def tile_moe_hie_none_kernel(tc, x_words, x_scales, wg, we_words, we_scales, gat
             queue = nc.sync if q < 2 else nc.scalar
             rows = x_scales[0, 4 * q : 4 * q + 4, :].bitcast(I32)
             queue.dma_start(
-                token_scales[QUADRANT * q : QUADRANT * (q + 1), :].bitcast(I32),
+                token_scales[QUADRANT * q : QUADRANT * (q + 1), 0:T].bitcast(I32),
                 rows.unsqueeze(0).broadcast_to([QUADRANT // 4, 4, T // 4]),
             )
 
@@ -77,17 +79,15 @@ def tile_moe_hie_none_kernel(tc, x_words, x_scales, wg, we_words, we_scales, gat
         for f, h in ((0, 1), (1, 0), (1, 1)):
             load_wg(f, h)
         nc.sync.dma_start(offs2_t[:], offs2)
+        nc.sync.dma_start(dst_t[:], dst)
+        nc.sync.dma_start(gate_t[:], gate)
         nc.sync.dma_start(we_w[:].bitcast(I32), we_words[:, 0].rearrange("e p b -> p e b").bitcast(I32))
         for r in range(4):
             nc.sync.dma_start(we_s[r:P:QUADRANT].bitcast(I32), we_scales[:, 0, r:16:4, :].rearrange("e q n -> q e n").bitcast(I32))
-        nc.sync.dma_start(dst_t[:], dst)
-        nc.sync.dma_start(gate_t[:], gate)
 
         slot_words = {}
-        slot_scales = [tile([P, C1], U8, "slot_scales%d" % f) for f in range(G)]
-
-        def gather_scales(f):
-            nc.vector.tensor_copy(slot_scales[f][:], token_scales[:].indirect(entries(offs_t, f * C1, C1)))
+        all_scales = tile([P, T], U8, "slot_scales")
+        slot_scales = [all_scales[:, f * C1 : (f + 1) * C1] for f in range(G)]
 
         def gather_words(first, count, tag=None):
             slot_words[first] = tile([P, count], U32, "slot_words%d" % first, tag)
@@ -97,23 +97,23 @@ def tile_moe_hie_none_kernel(tc, x_words, x_scales, wg, we_words, we_scales, gat
             start = max(s for s in slot_words if s <= first)
             return slot_words[start][:, first - start : first - start + C2]
 
-        wg_first = tile([P, 2 * H], BF16, "wg_first")
         wg_rest = tile([P, 2304], BF16, "wg_rest")
-        wg_bf = [[wg_first[:], wg_rest[:, 768:1792]], [wg_rest[:, 1280:2304], wg_rest[:, 0:1024]]]
+        wg_first = tile([P, 2 * H], BF16, "wg_first")
+        wg_in = [[wg_first[:], wg_rest[:, 768:1792]], [wg_rest[:, 1280:2304], wg_rest[:, 0:1024]]]
         wg_codes = [tile([P, H], U32, "wg_codes%d" % f) for f in range(G)]
         wg_scales = [tile([P, H], U8, "wg_scales%d" % f) for f in range(G)]
 
-        def round_wg(f, h, u, copy):
+        def round_wg(f, h, copy, target, t0, t1):
             m0, m1 = h * HALF // PACK, (h + 1) * HALF // PACK
             copy(
-                wg_bf[f][u].rearrange("p (t m j) -> p m j t", t=2, j=PACK)[:, m0:m1],
-                wg_raw[f][h][:].rearrange("p j (m t) -> p m j t", t=PACK)[:, :, :, 2 * u : 2 * u + 2],
+                target.rearrange("p (t m j) -> p m j t", t=t1 - t0, j=PACK)[:, m0:m1],
+                wg_raw[f][h][:].rearrange("p j (m t) -> p m j t", t=PACK)[:, :, :, t0:t1],
             )
 
         def quantise_wg(f):
             for u in range(2):
                 cols = slice(u * HALF, (u + 1) * HALF)
-                nc.vector.quantize_mx(wg_codes[f][:, cols].bitcast(FP8X4), wg_scales[f][:, cols], wg_bf[f][u])
+                nc.vector.quantize_mx(wg_codes[f][:, cols].bitcast(FP8X4), wg_scales[f][:, cols], wg_in[f][u])
 
         def first_level(f, u, c0):
             bank = a_psum.tile([P, 2, C2], F32, name="a_bank")
@@ -134,7 +134,7 @@ def tile_moe_hie_none_kernel(tc, x_words, x_scales, wg, we_words, we_scales, gat
                 bank[:].rearrange("p d s -> p s d"),
             )
 
-        def first_level_plane(d):
+        def plane_product(d):
             bank = a_psum.tile([P, C1], F32, name="a_bank")
             places = slice(P * (2 + d), P * (3 + d))
             for c0 in (0, C2):
@@ -147,7 +147,10 @@ def tile_moe_hie_none_kernel(tc, x_words, x_scales, wg, we_words, we_scales, gat
                     start=True,
                     stop=True,
                 )
-            nc.scalar.copy(planes[:, (1 + d) * C1 : (2 + d) * C1], bank[:])
+            return bank
+
+        def plane_copy(d):
+            nc.scalar.copy(planes[:, (1 + d) * C1 : (2 + d) * C1], banks[d][:])
 
         picked = {}
         a_bf = {}
@@ -164,9 +167,9 @@ def tile_moe_hie_none_kernel(tc, x_words, x_scales, wg, we_words, we_scales, gat
                 COPY,
             )
 
-        def join_pairs(e):
-            a_bf[e] = tile([P, PACK * C2], BF16, "a_bf%d" % e)
-            nc.scalar.copy(
+        def join_pairs(e, tag=None, copy=nc.scalar.copy):
+            a_bf[e] = tile([P, PACK * C2], BF16, "a_bf%d" % e, tag)
+            copy(
                 a_bf[e][:].bitcast(U32).rearrange("p (s u) -> p s u", u=2),
                 picked[e].rearrange("p u s -> p s u"),
             )
@@ -186,25 +189,23 @@ def tile_moe_hie_none_kernel(tc, x_words, x_scales, wg, we_words, we_scales, gat
                 stop=True,
             )
 
-        def scatter(first, count, copy):
+        def scatter(first, count, copy, tag=None):
             e, c0 = divmod(first, C2)
-            y = tile([P, count], F32, "y%d" % first)
+            y = tile([P, count], F32, "y%d" % first, tag)
             copy(y[:], y_banks[e][:, c0 : c0 + count])
             nc.vector.tensor_tensor(result[:].indirect(entries(dst_t, first, count)), y[:], gate_t[:, first : first + count], MULT)
 
-        gather_scales(0)
-        gather_scales(1)
-        gather_words(0, C1)
-        gather_words(C1, C2)
+        nc.vector.tensor_copy(all_scales[:], token_scales[:].indirect(offs_t[:]))
+        gather_words(0, C1 + C2)
         for h in range(2):
             for u in range(2):
-                round_wg(0, h, u, nc.scalar.copy)
+                round_wg(0, h, nc.scalar.copy, wg_in[0][u], 2 * u, 2 * u + 2)
         quantise_wg(0)
         gather_words(C1 + C2, C2, "wg_raw01")
-        round_wg(1, 0, 1, nc.scalar.copy)
-        round_wg(1, 0, 0, nc.vector.tensor_copy)
-        round_wg(1, 1, 0, nc.vector.tensor_copy)
-        round_wg(1, 1, 1, nc.vector.tensor_copy)
+        round_wg(1, 0, nc.scalar.copy, wg_in[1][1], 2, PACK)
+        round_wg(1, 0, nc.vector.tensor_copy, wg_in[1][0], 0, 2)
+        round_wg(1, 1, nc.vector.tensor_copy, wg_in[1][0], 0, 2)
+        round_wg(1, 1, nc.vector.tensor_copy, wg_in[1][1], 2, PACK)
         for u in range(2):
             for c0 in (0, C2):
                 first_level(0, u, c0)
@@ -219,25 +220,26 @@ def tile_moe_hie_none_kernel(tc, x_words, x_scales, wg, we_words, we_scales, gat
         picked2 = tile([P, 2, C2], U32, "picked2")
         picked[2] = picked2[:]
         gather_pairs(picked[2][:, 0, :], 2 * C2, C2, 0)
-        first_level_plane(0)
-        join_pairs(0)
+        banks = [plane_product(d) for d in range(2)]
+        plane_copy(0)
+        join_pairs(0, None, nc.gpsimd.tensor_copy)
         second_level(0)
-        picked3 = tile([P, 2, C2], U32, "picked3", "a_bf0")
+        plane_copy(1)
+        join_pairs(1, None, nc.gpsimd.tensor_copy)
+        second_level(1)
+        picked3 = tile([P, 2, C2], U32, "picked3", "a_codes0")
         picked[3] = picked3[:]
         gather_pairs(picked[3][:, 0, :], 3 * C2, C2, 0)
-        first_level_plane(1)
-        join_pairs(1)
-        second_level(1)
-        scatter(0, C2, nc.vector.tensor_copy)
         gather_plane(2, 0)
         gather_plane(2, 1)
-        gather_plane(3, 0)
-        join_pairs(2)
+        scatter(0, C2, nc.scalar.copy)
+        join_pairs(2, "a_scales0")
         second_level(2)
-        scatter(C2, C2, nc.scalar.copy)
+        gather_plane(3, 0)
         gather_plane(3, 1)
-        join_pairs(3)
+        scatter(C2, C2, nc.scalar.copy)
+        join_pairs(3, "a_codes1")
         second_level(3)
-        scatter(2 * C2, C2, nc.scalar.copy)
+        scatter(2 * C2, C2, nc.scalar.copy, "a_codes0")
         scatter(3 * C2, C2, nc.scalar.copy)
         nc.sync.dma_start(out, result[:])

@@ -79,11 +79,12 @@ def tile_moe_hie_none_kernel(tc, x_words, x_scales, wg, we_words, we_scales, gat
         for f, h in ((0, 1), (1, 0), (1, 1)):
             load_wg(f, h)
         nc.sync.dma_start(offs2_t[:], offs2)
-        nc.sync.dma_start(dst_t[:], dst)
-        nc.sync.dma_start(gate_t[:], gate)
         nc.sync.dma_start(we_w[:].bitcast(I32), we_words[:, 0].rearrange("e p b -> p e b").bitcast(I32))
         for r in range(4):
             nc.sync.dma_start(we_s[r:P:QUADRANT].bitcast(I32), we_scales[:, 0, r:16:4, :].rearrange("e q n -> q e n").bitcast(I32))
+
+        nc.sync.dma_start(dst_t[:], dst)
+        nc.sync.dma_start(gate_t[:], gate)
 
         slot_words = {}
         all_scales = tile([P, T], U8, "slot_scales")
@@ -225,21 +226,21 @@ def tile_moe_hie_none_kernel(tc, x_words, x_scales, wg, we_words, we_scales, gat
         join_pairs(0, None, nc.gpsimd.tensor_copy)
         second_level(0)
         plane_copy(1)
-        join_pairs(1, None, nc.gpsimd.tensor_copy)
+        join_pairs(1, "slot_words0")
         second_level(1)
-        picked3 = tile([P, 2, C2], U32, "picked3", "a_codes0")
+        picked3 = tile([P, 2, C2], U32, "picked3", "picked0")
         picked[3] = picked3[:]
         gather_pairs(picked[3][:, 0, :], 3 * C2, C2, 0)
         gather_plane(2, 0)
-        gather_plane(2, 1)
         scatter(0, C2, nc.scalar.copy)
-        join_pairs(2, "a_scales0")
-        second_level(2)
+        gather_plane(2, 1)
         gather_plane(3, 0)
-        gather_plane(3, 1)
+        join_pairs(2)
+        second_level(2)
         scatter(C2, C2, nc.scalar.copy)
-        join_pairs(3, "a_codes1")
+        gather_plane(3, 1)
+        join_pairs(3)
         second_level(3)
-        scatter(2 * C2, C2, nc.scalar.copy, "a_codes0")
+        scatter(2 * C2, C2, nc.scalar.copy)
         scatter(3 * C2, C2, nc.scalar.copy)
         nc.sync.dma_start(out, result[:])

@@ -14,6 +14,7 @@ U8 = mybir.dt.uint8
 FP8X4 = mybir.dt.float8_e4m3fn_x4
 FP4X4 = mybir.dt.float4_e2m1fn_x4
 MULT = mybir.AluOpType.mult
+ADD = mybir.AluOpType.add
 COPY = mybir.ActivationFunctionType.Copy
 
 P = 128
@@ -98,9 +99,7 @@ def tile_moe_hie_none_kernel(tc, x_words, x_scales, wg, we_words, we_scales, gat
             start = max(s for s in slot_words if s <= first)
             return slot_words[start][:, first - start : first - start + C2]
 
-        wg_rest = tile([P, 2304], BF16, "wg_rest")
-        wg_first = tile([P, 2 * H], BF16, "wg_first")
-        wg_in = [[wg_first[:], wg_rest[:, 768:1792]], [wg_rest[:, 1280:2304], wg_rest[:, 0:1024]]]
+        wg_in = [[tile([P, 2 * H], BF16, "wg_in%d%d" % (f, u))[:] for u in range(2)] for f in range(G)]
         wg_codes = [tile([P, H], U32, "wg_codes%d" % f) for f in range(G)]
         wg_scales = [tile([P, H], U8, "wg_scales%d" % f) for f in range(G)]
 
@@ -198,13 +197,21 @@ def tile_moe_hie_none_kernel(tc, x_words, x_scales, wg, we_words, we_scales, gat
 
         nc.vector.tensor_copy(all_scales[:], token_scales[:].indirect(offs_t[:]))
         gather_words(0, C1 + C2)
-        for h in range(2):
-            for u in range(2):
-                round_wg(0, h, nc.scalar.copy, wg_in[0][u], 2 * u, 2 * u + 2)
+        round_wg(0, 0, nc.scalar.copy, wg_in[0][0], 0, 2)
+        round_wg(0, 0, nc.scalar.copy, wg_in[0][1], 2, PACK)
+        round_wg(0, 1, nc.scalar.copy, wg_in[0][0], 0, 2)
+        nc.gpsimd.tensor_scalar(
+            wg_in[0][1].rearrange("p (t m j) -> p m t j", t=2, j=PACK)[:, HALF // PACK :],
+            wg_raw[0][1][:].rearrange("p j (m t) -> p m t j", t=PACK)[:, :, 2:PACK],
+            1.0,
+            0.0,
+            MULT,
+            ADD,
+        )
         quantise_wg(0)
         gather_words(C1 + C2, C2, "wg_raw01")
         round_wg(1, 0, nc.scalar.copy, wg_in[1][1], 2, PACK)
-        round_wg(1, 0, nc.vector.tensor_copy, wg_in[1][0], 0, 2)
+        round_wg(1, 0, nc.scalar.copy, wg_in[1][0], 0, 2)
         round_wg(1, 1, nc.vector.tensor_copy, wg_in[1][0], 0, 2)
         round_wg(1, 1, nc.vector.tensor_copy, wg_in[1][1], 2, PACK)
         for u in range(2):

@@ -25,6 +25,7 @@ HALF = H // 2
 SCALE_SPARE = 384
 SPARE = 256
 SHARED = 256
+PIECES = ((0, 0, 64), (0, 64, 128), (1, 0, 64), (1, 64, 96), (1, 96, 128))
 A_BANKS, Y_BANKS = 6, 2
 
 
@@ -46,7 +47,7 @@ def tile_moe_hie_none_kernel(tc, x_words, x_scales, wg, we_words, we_scales, gat
         dst_t = tile([P, T // PER_COLUMN], U16, "dst_t")
         token_words = tile([P, T], I32, "token_words")
         token_scales = tile([P, T + SCALE_SPARE], U8, "token_scales")
-        wg_raw = [[tile([P, PACK, HALF], F32, "wg_raw%d%d" % (f, h)) for h in range(2)] for f in range(G)]
+        wg_raw = {(f, m0): tile([P, PACK, PACK * (m1 - m0)], F32, "wg_raw%d_%d" % (f, m0)) for f, m0, m1 in PIECES}
         we_w = tile([P, E, 2 * N], U8, "we_w")
         we_s = tile([P, E, N], U8, "we_s")
         gate_t = tile([P, T], F32, "gate_t")
@@ -72,13 +73,13 @@ def tile_moe_hie_none_kernel(tc, x_words, x_scales, wg, we_words, we_scales, gat
                 rows.unsqueeze(0).broadcast_to([QUADRANT // 4, 4, T // 4]),
             )
 
-        def load_wg(f, h):
-            nc.sync.dma_start(wg_raw[f][h][:], wg[f].rearrange("(p j) c -> p j c", j=PACK)[:, :, HALF * h : HALF * (h + 1)])
+        def load_wg(f, m0, m1):
+            nc.sync.dma_start(wg_raw[f, m0][:], wg[f].rearrange("(p j) c -> p j c", j=PACK)[:, :, PACK * m0 : PACK * m1])
 
-        load_wg(0, 0)
+        load_wg(*PIECES[0])
         nc.sync.dma_start(token_words[:], x_words[0].rearrange("p t d -> p (t d)").bitcast(I32))
-        for f, h in ((0, 1), (1, 0), (1, 1)):
-            load_wg(f, h)
+        for piece in PIECES[1:]:
+            load_wg(*piece)
         nc.sync.dma_start(offs2_t[:], offs2)
         nc.sync.dma_start(we_w[:].bitcast(I32), we_words[:, 0].rearrange("e p b -> p e b").bitcast(I32))
         for r in range(4):
@@ -99,16 +100,26 @@ def tile_moe_hie_none_kernel(tc, x_words, x_scales, wg, we_words, we_scales, gat
             start = max(s for s in slot_words if s <= first)
             return slot_words[start][:, first - start : first - start + C2]
 
-        wg_in = [[tile([P, 2 * H], BF16, "wg_in%d%d" % (f, u))[:] for u in range(2)] for f in range(G)]
+        wg_shared = tile([P, 768 + 2 * H], BF16, "wg_shared")
+        wg_late = tile([P, 768 + 2 * H], BF16, "wg_late")
+        wg_in = [
+            [wg_late[:, 768:], wg_shared[:, 768:]],
+            [wg_shared[:, 0 : 2 * H], wg_late[:, 0 : 2 * H]],
+        ]
         wg_codes = [tile([P, H], U32, "wg_codes%d" % f) for f in range(G)]
         wg_scales = [tile([P, H], U8, "wg_scales%d" % f) for f in range(G)]
 
-        def round_wg(f, h, copy, target, t0, t1):
-            m0, m1 = h * HALF // PACK, (h + 1) * HALF // PACK
-            copy(
-                target.rearrange("p (t m j) -> p m j t", t=t1 - t0, j=PACK)[:, m0:m1],
-                wg_raw[f][h][:].rearrange("p j (m t) -> p m j t", t=PACK)[:, :, :, t0:t1],
-            )
+        def views(f, u, m0, m1, walk):
+            start = max(s for g, s, end in PIECES if g == f and s <= m0)
+            target = wg_in[f][u].rearrange("p (t m j) -> p m t j", t=2, j=PACK)[:, m0:m1]
+            source = wg_raw[f, start][:].rearrange("p j (m t) -> p m t j", t=PACK)[:, m0 - start : m1 - start, 2 * u : 2 * u + 2]
+            return target.rearrange("p m t j -> " + walk), source.rearrange("p m t j -> " + walk)
+
+        def round_wg(copy, f, u, m0, m1):
+            copy(*views(f, u, m0, m1, "p m j t"))
+
+        def round_on_gpsimd(f, u, m0, m1):
+            nc.gpsimd.tensor_scalar(*views(f, u, m0, m1, "p m t j"), 1.0, 0.0, MULT, ADD)
 
         def quantise_wg(f):
             for u in range(2):
@@ -197,23 +208,17 @@ def tile_moe_hie_none_kernel(tc, x_words, x_scales, wg, we_words, we_scales, gat
 
         nc.vector.tensor_copy(all_scales[:], token_scales[:].indirect(offs_t[:]))
         gather_words(0, C1 + C2)
-        round_wg(0, 0, nc.scalar.copy, wg_in[0][0], 0, 2)
-        round_wg(0, 0, nc.scalar.copy, wg_in[0][1], 2, PACK)
-        round_wg(0, 1, nc.scalar.copy, wg_in[0][0], 0, 2)
-        nc.gpsimd.tensor_scalar(
-            wg_in[0][1].rearrange("p (t m j) -> p m t j", t=2, j=PACK)[:, HALF // PACK :],
-            wg_raw[0][1][:].rearrange("p j (m t) -> p m t j", t=PACK)[:, :, 2:PACK],
-            1.0,
-            0.0,
-            MULT,
-            ADD,
-        )
+        round_wg(nc.scalar.copy, 0, 0, 0, 64)
+        round_wg(nc.scalar.copy, 0, 1, 0, 64)
+        round_wg(nc.scalar.copy, 0, 0, 64, 128)
+        round_on_gpsimd(0, 1, 64, 128)
         quantise_wg(0)
-        gather_words(C1 + C2, C2, "wg_raw01")
-        round_wg(1, 0, nc.scalar.copy, wg_in[1][1], 2, PACK)
-        round_wg(1, 0, nc.scalar.copy, wg_in[1][0], 0, 2)
-        round_wg(1, 1, nc.vector.tensor_copy, wg_in[1][0], 0, 2)
-        round_wg(1, 1, nc.vector.tensor_copy, wg_in[1][1], 2, PACK)
+        gather_words(C1 + C2, C2, "wg_raw0_64")
+        round_wg(nc.scalar.copy, 1, 1, 0, 64)
+        round_wg(nc.scalar.copy, 1, 0, 0, 64)
+        for m0 in (64, 96):
+            for u in range(2):
+                round_wg(nc.vector.tensor_copy, 1, u, m0, m0 + 32)
         for u in range(2):
             for c0 in (0, C2):
                 first_level(0, u, c0)

@@ -23,9 +23,8 @@ QUADRANT = 32
 PER_COLUMN = 16
 HALF = H // 2
 SCALE_SPARE = 384
-SPARE = 256
 SHARED = 256
-PIECES = ((0, 0, 64), (0, 64, 128), (1, 0, 64), (1, 64, 96), (1, 96, 128))
+PIECES = ((0, 0, 64), (0, 64, 128), (1, 0, 64), (1, 64, 128))
 A_BANKS, Y_BANKS = 6, 2
 
 
@@ -50,19 +49,13 @@ def tile_moe_hie_none_kernel(tc, x_words, x_scales, wg, we_words, we_scales, gat
         wg_raw = {(f, m0): tile([P, PACK, PACK * (m1 - m0)], F32, "wg_raw%d_%d" % (f, m0)) for f, m0, m1 in PIECES}
         we_w = tile([P, E, 2 * N], U8, "we_w")
         we_s = tile([P, E, N], U8, "we_s")
-        gate_t = tile([P, T], F32, "gate_t")
-        pairs = [
-            [tile([P, 2 * (C1 + SPARE)], BF16, "pairs00"), tile([P, 2 * C1], BF16, "pairs01")],
-            [tile([P, 2 * T], BF16, "pairs10")],
-        ]
-        planes = tile([P, 3 * C1], BF16, "planes")
+        work = tile([P, 4 * C2 + T], F32, "work")
+        gate_t = work[:, 4 * C2 :]
+        pairs = [tile([P, 2 * T], BF16, "pairs%d" % u) for u in range(2)]
         result = tile([P, T], F32, "result")
 
         nc.vector.memset(we_s[:].rearrange("p e n -> p (e n)").bitcast(I32), 0)
         nc.vector.memset(token_scales[:, T:].bitcast(I32), 0)
-        nc.vector.memset(pairs[0][0][:, 2 * C1 :].bitcast(I32), 0)
-        nc.vector.memset(pairs[1][0][:, 0 : 2 * C1].bitcast(I32), 0)
-        nc.vector.memset(planes[:, 0:C1].bitcast(I32), 0)
 
         nc.sync.dma_start(offs_t[:], offs)
         for q in range(P // QUADRANT):
@@ -81,12 +74,12 @@ def tile_moe_hie_none_kernel(tc, x_words, x_scales, wg, we_words, we_scales, gat
         for piece in PIECES[1:]:
             load_wg(*piece)
         nc.sync.dma_start(offs2_t[:], offs2)
+        nc.sync.dma_start(gate_t, gate)
         nc.sync.dma_start(we_w[:].bitcast(I32), we_words[:, 0].rearrange("e p b -> p e b").bitcast(I32))
         for r in range(4):
             nc.sync.dma_start(we_s[r:P:QUADRANT].bitcast(I32), we_scales[:, 0, r:16:4, :].rearrange("e q n -> q e n").bitcast(I32))
 
         nc.sync.dma_start(dst_t[:], dst)
-        nc.sync.dma_start(gate_t[:], gate)
 
         slot_words = {}
         all_scales = tile([P, T], U8, "slot_scales")
@@ -100,11 +93,11 @@ def tile_moe_hie_none_kernel(tc, x_words, x_scales, wg, we_words, we_scales, gat
             start = max(s for s in slot_words if s <= first)
             return slot_words[start][:, first - start : first - start + C2]
 
-        wg_shared = tile([P, 768 + 2 * H], BF16, "wg_shared")
+        wg_shared = tile([P, 2 * H], BF16, "wg_shared")
         wg_late = tile([P, 768 + 2 * H], BF16, "wg_late")
         wg_in = [
-            [wg_late[:, 768:], wg_shared[:, 768:]],
-            [wg_shared[:, 0 : 2 * H], wg_late[:, 0 : 2 * H]],
+            [wg_late[:, 768:], wg_shared[:]],
+            [wg_shared[:], wg_late[:, 0 : 2 * H]],
         ]
         wg_codes = [tile([P, H], U32, "wg_codes%d" % f) for f in range(G)]
         wg_scales = [tile([P, H], U8, "wg_scales%d" % f) for f in range(G)]
@@ -141,54 +134,38 @@ def tile_moe_hie_none_kernel(tc, x_words, x_scales, wg, we_words, we_scales, gat
                     stop=True,
                 )
             nc.scalar.copy(
-                pairs[f][u][:].rearrange("p (s d) -> p s d", d=2)[:, first : first + C2, :],
+                pairs[u][:].rearrange("p (s d) -> p s d", d=2)[:, first : first + C2, :],
                 bank[:].rearrange("p d s -> p s d"),
             )
 
-        def plane_product(d):
-            bank = a_psum.tile([P, C1], F32, name="a_bank")
-            places = slice(P * (2 + d), P * (3 + d))
-            for c0 in (0, C2):
-                nc.tensor.matmul_mx(
-                    bank[:, c0 : c0 + C2],
-                    lhsT=wg_codes[1][:, places].bitcast(FP8X4),
-                    lhsT_scale=wg_scales[1][:, places],
-                    rhs=words_of(C1 + c0).bitcast(FP8X4),
-                    rhs_scale=slot_scales[1][:, c0 : c0 + C2],
-                    start=True,
-                    stop=True,
-                )
-            return bank
+        def work_runs(first):
+            return work[:, first * C2 : (first + 2) * C2]
 
-        def plane_copy(d):
-            nc.scalar.copy(planes[:, (1 + d) * C1 : (2 + d) * C1], banks[d][:])
-
-        picked = {}
-        a_bf = {}
+        picked1 = tile([P, 2 * C2], U32, "picked1")
+        picked = [work_runs(2).bitcast(U32), picked1[:], work_runs(3).bitcast(U32), work_runs(2).bitcast(U32)]
+        a_bf2 = tile([P, PACK * C2], BF16, "a_bf2")
+        a_bf3 = tile([P, PACK * C2], BF16, "a_bf3")
+        a_bf = [work_runs(0).bitcast(BF16), work_runs(1).bitcast(BF16), a_bf2[:], a_bf3[:]]
         y_banks = {}
+        gated = {}
 
-        def gather_pairs(target, first, count, u):
-            f = first // C1
-            nc.vector.tensor_copy(target, pairs[f][u][:].bitcast(U32).indirect(entries(offs2_t, first, count)))
+        def runs(e):
+            return picked[e]
 
-        def gather_plane(e, d):
-            nc.scalar.activation(
-                picked[e][:, 1, :].bitcast(BF16).rearrange("p (s d) -> p s d", d=2)[:, :, d],
-                planes[:, d * C1 : d * C1 + T].indirect(entries(offs2_t, e * C2, C2)),
-                COPY,
-            )
+        def gather_pairs(e, u):
+            window = pairs[u][:].bitcast(U32)[:, 0 : (e // 2 + 1) * C1]
+            nc.vector.tensor_copy(runs(e)[:, u * C2 : (u + 1) * C2], window.indirect(entries(offs2_t, e * C2, C2)))
 
-        def join_pairs(e, tag=None, copy=nc.scalar.copy):
-            a_bf[e] = tile([P, PACK * C2], BF16, "a_bf%d" % e, tag)
+        def join_pairs(e, copy):
             copy(
-                a_bf[e][:].bitcast(U32).rearrange("p (s u) -> p s u", u=2),
-                picked[e].rearrange("p u s -> p s u"),
+                a_bf[e].bitcast(U32).rearrange("p (s u) -> p s u", u=2),
+                runs(e).rearrange("p (u s) -> p s u", u=2),
             )
 
-        def second_level(e):
-            a_codes = tile([P, C2], U32, "a_codes%d" % e)
+        def second_level(e, tag=None):
+            a_codes = tile([P, C2], U32, "a_codes%d" % e, tag)
             a_scales = tile([P, C2], U8, "a_scales%d" % e)
-            nc.vector.quantize_mx(a_codes[:].bitcast(FP8X4), a_scales[:], a_bf[e][:])
+            nc.vector.quantize_mx(a_codes[:].bitcast(FP8X4), a_scales[:], a_bf[e])
             y_banks[e] = y_psum.tile([P, C2], F32, name="y_bank")
             nc.tensor.matmul_mx(
                 y_banks[e][:],
@@ -200,11 +177,12 @@ def tile_moe_hie_none_kernel(tc, x_words, x_scales, wg, we_words, we_scales, gat
                 stop=True,
             )
 
-        def scatter(first, count, copy, tag=None):
-            e, c0 = divmod(first, C2)
-            y = tile([P, count], F32, "y%d" % first, tag)
-            copy(y[:], y_banks[e][:, c0 : c0 + count])
-            nc.vector.tensor_tensor(result[:].indirect(entries(dst_t, first, count)), y[:], gate_t[:, first : first + count], MULT)
+        def apply_gate(e):
+            gated[e] = tile([P, C2], F32, "gated%d" % e)
+            nc.vector.tensor_tensor(gated[e][:], y_banks[e][:], gate_t[:, e * C2 : (e + 1) * C2], MULT)
+
+        def scatter(e):
+            nc.scalar.activation(result[:].indirect(entries(dst_t, e * C2, C2)), gated[e][:], COPY)
 
         nc.vector.tensor_copy(all_scales[:], token_scales[:].indirect(offs_t[:]))
         gather_words(0, C1 + C2)
@@ -215,44 +193,39 @@ def tile_moe_hie_none_kernel(tc, x_words, x_scales, wg, we_words, we_scales, gat
         quantise_wg(0)
         gather_words(C1 + C2, C2, "wg_raw0_64")
         round_wg(nc.scalar.copy, 1, 1, 0, 64)
-        round_wg(nc.scalar.copy, 1, 0, 0, 64)
-        for m0 in (64, 96):
-            for u in range(2):
-                round_wg(nc.vector.tensor_copy, 1, u, m0, m0 + 32)
+        round_on_gpsimd(1, 0, 0, 64)
+        for u in range(2):
+            round_wg(nc.vector.tensor_copy, 1, u, 64, 128)
         for u in range(2):
             for c0 in (0, C2):
                 first_level(0, u, c0)
         quantise_wg(1)
-        picked0 = tile([P, 2, C1], U32, "picked0")
-        picked[0], picked[1] = picked0[:, :, 0:C2], picked0[:, :, C2:C1]
-        gather_pairs(picked0[:, 0, :], 0, C1, 0)
-        gather_pairs(picked[0][:, 1, :], 0, C2, 1)
-        gather_pairs(picked[1][:, 1, :], C2, C2, 1)
+        gather_pairs(0, 0)
+        gather_pairs(1, 0)
+        gather_pairs(0, 1)
+        gather_pairs(1, 1)
         first_level(1, 0, 0)
         first_level(1, 0, C2)
-        picked2 = tile([P, 2, C2], U32, "picked2")
-        picked[2] = picked2[:]
-        gather_pairs(picked[2][:, 0, :], 2 * C2, C2, 0)
-        banks = [plane_product(d) for d in range(2)]
-        plane_copy(0)
-        join_pairs(0, None, nc.gpsimd.tensor_copy)
+        join_pairs(0, nc.scalar.copy)
         second_level(0)
-        plane_copy(1)
-        join_pairs(1, "slot_words0")
-        second_level(1)
-        picked3 = tile([P, 2, C2], U32, "picked3", "picked0")
-        picked[3] = picked3[:]
-        gather_pairs(picked[3][:, 0, :], 3 * C2, C2, 0)
-        gather_plane(2, 0)
-        scatter(0, C2, nc.scalar.copy)
-        gather_plane(2, 1)
-        gather_plane(3, 0)
-        join_pairs(2)
+        join_pairs(1, nc.gpsimd.tensor_copy)
+        first_level(1, 1, 0)
+        first_level(1, 1, C2)
+        gather_pairs(2, 0)
+        apply_gate(0)
+        scatter(0)
+        second_level(1, "a_codes0")
+        gather_pairs(2, 1)
+        join_pairs(2, nc.gpsimd.tensor_copy)
+        gather_pairs(3, 0)
+        apply_gate(1)
+        scatter(1)
         second_level(2)
-        scatter(C2, C2, nc.scalar.copy)
-        gather_plane(3, 1)
-        join_pairs(3)
+        gather_pairs(3, 1)
+        join_pairs(3, nc.gpsimd.tensor_copy)
+        apply_gate(2)
+        scatter(2)
         second_level(3)
-        scatter(2 * C2, C2, nc.scalar.copy)
-        scatter(3 * C2, C2, nc.scalar.copy)
+        apply_gate(3)
+        scatter(3)
         nc.sync.dma_start(out, result[:])

@@ -49,8 +49,8 @@ def tile_moe_hie_none_kernel(tc, x_words, x_scales, wg, we_words, we_scales, gat
         wg_raw = {(f, m0): tile([P, PACK, PACK * (m1 - m0)], F32, "wg_raw%d_%d" % (f, m0)) for f, m0, m1 in PIECES}
         we_w = tile([P, E, 2 * N], U8, "we_w")
         we_s = tile([P, E, N], U8, "we_s")
-        work = tile([P, 4 * C2 + T], F32, "work")
-        gate_t = work[:, 4 * C2 :]
+        work = tile([P, 2 * C2 + T], F32, "work")
+        gate_t = work[:, 2 * C2 :]
         pairs = [tile([P, 2 * T], BF16, "pairs%d" % u) for u in range(2)]
         result = tile([P, T], F32, "result")
 
@@ -93,11 +93,11 @@ def tile_moe_hie_none_kernel(tc, x_words, x_scales, wg, we_words, we_scales, gat
             start = max(s for s in slot_words if s <= first)
             return slot_words[start][:, first - start : first - start + C2]
 
-        wg_shared = tile([P, 2 * H], BF16, "wg_shared")
+        wg_shared = tile([P, 768 + 2 * H], BF16, "wg_shared")
         wg_late = tile([P, 768 + 2 * H], BF16, "wg_late")
         wg_in = [
-            [wg_late[:, 768:], wg_shared[:]],
-            [wg_shared[:], wg_late[:, 0 : 2 * H]],
+            [wg_late[:, 768:], wg_shared[:, 768:]],
+            [wg_shared[:, 0 : 2 * H], wg_late[:, 0 : 2 * H]],
         ]
         wg_codes = [tile([P, H], U32, "wg_codes%d" % f) for f in range(G)]
         wg_scales = [tile([P, H], U8, "wg_scales%d" % f) for f in range(G)]
@@ -142,10 +142,8 @@ def tile_moe_hie_none_kernel(tc, x_words, x_scales, wg, we_words, we_scales, gat
             return work[:, first * C2 : (first + 2) * C2]
 
         picked1 = tile([P, 2 * C2], U32, "picked1")
-        picked = [work_runs(2).bitcast(U32), picked1[:], work_runs(3).bitcast(U32), work_runs(2).bitcast(U32)]
-        a_bf2 = tile([P, PACK * C2], BF16, "a_bf2")
-        a_bf3 = tile([P, PACK * C2], BF16, "a_bf3")
-        a_bf = [work_runs(0).bitcast(BF16), work_runs(1).bitcast(BF16), a_bf2[:], a_bf3[:]]
+        picked = [work_runs(0).bitcast(U32), picked1[:], work_runs(1).bitcast(U32), work_runs(2).bitcast(U32)]
+        a_bf = {}
         y_banks = {}
         gated = {}
 
@@ -156,15 +154,16 @@ def tile_moe_hie_none_kernel(tc, x_words, x_scales, wg, we_words, we_scales, gat
             window = pairs[u][:].bitcast(U32)[:, 0 : (e // 2 + 1) * C1]
             nc.vector.tensor_copy(runs(e)[:, u * C2 : (u + 1) * C2], window.indirect(entries(offs2_t, e * C2, C2)))
 
-        def join_pairs(e, copy):
+        def join_pairs(e, copy, tag=None):
+            a_bf[e] = tile([P, PACK * C2], BF16, "a_bf%d" % e, tag)[:]
             copy(
                 a_bf[e].bitcast(U32).rearrange("p (s u) -> p s u", u=2),
                 runs(e).rearrange("p (u s) -> p s u", u=2),
             )
 
         def second_level(e, tag=None):
-            a_codes = tile([P, C2], U32, "a_codes%d" % e, tag)
-            a_scales = tile([P, C2], U8, "a_scales%d" % e)
+            a_codes = tile([P, C2], U32, "a_codes%d" % e)
+            a_scales = tile([P, C2], U8, "a_scales%d" % e, tag)
             nc.vector.quantize_mx(a_codes[:].bitcast(FP8X4), a_scales[:], a_bf[e])
             y_banks[e] = y_psum.tile([P, C2], F32, name="y_bank")
             nc.tensor.matmul_mx(
@@ -184,6 +183,9 @@ def tile_moe_hie_none_kernel(tc, x_words, x_scales, wg, we_words, we_scales, gat
         def scatter(e):
             nc.scalar.activation(result[:].indirect(entries(dst_t, e * C2, C2)), gated[e][:], COPY)
 
+        def scatter_on_vector(e):
+            nc.vector.tensor_copy(result[:].indirect(entries(dst_t, e * C2, C2)), gated[e][:])
+
         nc.vector.tensor_copy(all_scales[:], token_scales[:].indirect(offs_t[:]))
         gather_words(0, C1 + C2)
         round_wg(nc.scalar.copy, 0, 0, 0, 64)
@@ -193,7 +195,7 @@ def tile_moe_hie_none_kernel(tc, x_words, x_scales, wg, we_words, we_scales, gat
         quantise_wg(0)
         gather_words(C1 + C2, C2, "wg_raw0_64")
         round_wg(nc.scalar.copy, 1, 1, 0, 64)
-        round_on_gpsimd(1, 0, 0, 64)
+        round_wg(nc.scalar.copy, 1, 0, 0, 64)
         for u in range(2):
             round_wg(nc.vector.tensor_copy, 1, u, 64, 128)
         for u in range(2):
@@ -208,24 +210,24 @@ def tile_moe_hie_none_kernel(tc, x_words, x_scales, wg, we_words, we_scales, gat
         first_level(1, 0, C2)
         join_pairs(0, nc.scalar.copy)
         second_level(0)
-        join_pairs(1, nc.gpsimd.tensor_copy)
+        join_pairs(1, nc.scalar.copy)
         first_level(1, 1, 0)
         first_level(1, 1, C2)
         gather_pairs(2, 0)
         apply_gate(0)
         scatter(0)
-        second_level(1, "a_codes0")
+        second_level(1, "a_scales0")
         gather_pairs(2, 1)
-        join_pairs(2, nc.gpsimd.tensor_copy)
-        gather_pairs(3, 0)
         apply_gate(1)
         scatter(1)
-        second_level(2)
+        join_pairs(2, nc.vector.tensor_copy, "a_codes1")
         gather_pairs(3, 1)
-        join_pairs(3, nc.gpsimd.tensor_copy)
+        second_level(2)
+        gather_pairs(3, 0)
         apply_gate(2)
         scatter(2)
+        join_pairs(3, nc.vector.tensor_copy, "a_codes2")
         second_level(3)
         apply_gate(3)
-        scatter(3)
+        scatter_on_vector(3)
         nc.sync.dma_start(out, result[:])

@@ -74,11 +74,13 @@ def tile_moe_hie_none_kernel(tc, x_words, x_scales, wg, we_words, we_scales, gat
         for piece in PIECES[1:]:
             load_wg(*piece)
         nc.sync.dma_start(offs2_t[:], offs2)
-        nc.sync.dma_start(gate_t, gate)
         nc.sync.dma_start(we_w[:].bitcast(I32), we_words[:, 0].rearrange("e p b -> p e b").bitcast(I32))
         for r in range(4):
+            if r == 3:
+                nc.sync.dma_start(gate_t[:, 0:C2], gate[:, 0:C2])
             nc.sync.dma_start(we_s[r:P:QUADRANT].bitcast(I32), we_scales[:, 0, r:16:4, :].rearrange("e q n -> q e n").bitcast(I32))
 
+        nc.sync.dma_start(gate_t[:, C2:], gate[:, C2:])
         nc.sync.dma_start(dst_t[:], dst)
 
         slot_words = {}

@@ -49,13 +49,17 @@ def tile_moe_hie_none_kernel(tc, x_words, x_scales, wg, we_words, we_scales, gat
         wg_raw = {(f, m0): tile([P, PACK, PACK * (m1 - m0)], F32, "wg_raw%d_%d" % (f, m0)) for f, m0, m1 in PIECES}
         we_w = tile([P, E, 2 * N], U8, "we_w")
         we_s = tile([P, E, N], U8, "we_s")
-        work = tile([P, 2 * C2 + T], F32, "work")
-        gate_t = work[:, 2 * C2 :]
+        work = tile([P, 3 * C2 + T], F32, "work")
+        gate_t = work[:, 3 * C2 :]
         pairs = [tile([P, 2 * T], BF16, "pairs%d" % u) for u in range(2)]
+        by_scalar = tile([P, T], F32, "by_scalar")
+        by_vector = tile([P, T], F32, "by_vector")
         result = tile([P, T], F32, "result")
 
         nc.vector.memset(we_s[:].rearrange("p e n -> p (e n)").bitcast(I32), 0)
         nc.vector.memset(token_scales[:, T:].bitcast(I32), 0)
+        nc.vector.memset(by_scalar[:].bitcast(I32), 0)
+        nc.vector.memset(by_vector[:].bitcast(I32), 0)
 
         nc.sync.dma_start(offs_t[:], offs)
         for q in range(P // QUADRANT):
@@ -144,7 +148,7 @@ def tile_moe_hie_none_kernel(tc, x_words, x_scales, wg, we_words, we_scales, gat
             return work[:, first * C2 : (first + 2) * C2]
 
         picked1 = tile([P, 2 * C2], U32, "picked1")
-        picked = [work_runs(0).bitcast(U32), picked1[:], work_runs(1).bitcast(U32), work_runs(2).bitcast(U32)]
+        picked = [work_runs(1).bitcast(U32), picked1[:], work_runs(2).bitcast(U32), work_runs(1).bitcast(U32)]
         a_bf = {}
         y_banks = {}
         gated = {}
@@ -156,8 +160,8 @@ def tile_moe_hie_none_kernel(tc, x_words, x_scales, wg, we_words, we_scales, gat
             window = pairs[u][:].bitcast(U32)[:, 0 : (e // 2 + 1) * C1]
             nc.vector.tensor_copy(runs(e)[:, u * C2 : (u + 1) * C2], window.indirect(entries(offs2_t, e * C2, C2)))
 
-        def join_pairs(e, copy, tag=None):
-            a_bf[e] = tile([P, PACK * C2], BF16, "a_bf%d" % e, tag)[:]
+        def join_pairs(e, copy):
+            a_bf[e] = work_runs(0).bitcast(BF16) if e == 1 else tile([P, PACK * C2], BF16, "a_bf%d" % e)[:]
             copy(
                 a_bf[e].bitcast(U32).rearrange("p (s u) -> p s u", u=2),
                 runs(e).rearrange("p (u s) -> p s u", u=2),
@@ -182,11 +186,11 @@ def tile_moe_hie_none_kernel(tc, x_words, x_scales, wg, we_words, we_scales, gat
             gated[e] = tile([P, C2], F32, "gated%d" % e)
             nc.vector.tensor_tensor(gated[e][:], y_banks[e][:], gate_t[:, e * C2 : (e + 1) * C2], MULT)
 
-        def scatter(e):
-            nc.scalar.activation(result[:].indirect(entries(dst_t, e * C2, C2)), gated[e][:], COPY)
+        def scatter(e, c0=0, count=C2):
+            nc.scalar.activation(by_scalar[:].indirect(entries(dst_t, e * C2 + c0, count)), gated[e][:, c0 : c0 + count], COPY)
 
-        def scatter_on_vector(e):
-            nc.vector.tensor_copy(result[:].indirect(entries(dst_t, e * C2, C2)), gated[e][:])
+        def scatter_on_vector(e, c0, count):
+            nc.vector.tensor_copy(by_vector[:].indirect(entries(dst_t, e * C2 + c0, count)), gated[e][:, c0 : c0 + count])
 
         nc.vector.tensor_copy(all_scales[:], token_scales[:].indirect(offs_t[:]))
         gather_words(0, C1 + C2)
@@ -220,16 +224,20 @@ def tile_moe_hie_none_kernel(tc, x_words, x_scales, wg, we_words, we_scales, gat
         scatter(0)
         second_level(1, "a_scales0")
         gather_pairs(2, 1)
+        join_pairs(2, nc.gpsimd.tensor_copy)
+        gather_pairs(3, 0)
         apply_gate(1)
         scatter(1)
-        join_pairs(2, nc.vector.tensor_copy, "a_codes1")
-        gather_pairs(3, 1)
         second_level(2)
-        gather_pairs(3, 0)
+        gather_pairs(3, 1)
+        join_pairs(3, nc.vector.tensor_copy)
         apply_gate(2)
-        scatter(2)
-        join_pairs(3, nc.vector.tensor_copy, "a_codes2")
+        scatter(2, 0, P)
         second_level(3)
+        scatter_on_vector(2, P, P)
         apply_gate(3)
-        scatter_on_vector(3)
-        nc.sync.dma_start(out, result[:])
+        scatter(3, 0, P)
+        scatter_on_vector(3, P, P)
+        for c0 in (0, C1):
+            nc.vector.tensor_tensor(result[:, c0 : c0 + C1], by_scalar[:, c0 : c0 + C1], by_vector[:, c0 : c0 + C1], ADD)
+            nc.sync.dma_start(out[:, c0 : c0 + C1], result[:, c0 : c0 + C1])

@@ -238,6 +238,6 @@ def tile_moe_hie_none_kernel(tc, x_words, x_scales, wg, we_words, we_scales, gat
         apply_gate(3)
         scatter(3, 0, P)
         scatter_on_vector(3, P, P)
-        for c0 in (0, C1):
-            nc.vector.tensor_tensor(result[:, c0 : c0 + C1], by_scalar[:, c0 : c0 + C1], by_vector[:, c0 : c0 + C1], ADD)
-            nc.sync.dma_start(out[:, c0 : c0 + C1], result[:, c0 : c0 + C1])
+        for c0, c1 in ((0, 256), (256, 512), (512, 768), (768, 1024)):
+            nc.vector.tensor_tensor(result[:, c0:c1], by_scalar[:, c0:c1], by_vector[:, c0:c1], ADD)
+            nc.sync.dma_start(out[:, c0:c1], result[:, c0:c1])

@@ -49,8 +49,8 @@ def tile_moe_hie_none_kernel(tc, x_words, x_scales, wg, we_words, we_scales, gat
         wg_raw = {(f, m0): tile([P, PACK, PACK * (m1 - m0)], F32, "wg_raw%d_%d" % (f, m0)) for f, m0, m1 in PIECES}
         we_w = tile([P, E, 2 * N], U8, "we_w")
         we_s = tile([P, E, N], U8, "we_s")
-        work = tile([P, 3 * C2 + T], F32, "work")
-        gate_t = work[:, 3 * C2 :]
+        work = tile([P, 6 * C2 + T], F32, "work")
+        gate_t = work[:, 4 * C2 : 4 * C2 + T]
         pairs = [tile([P, 2 * T], BF16, "pairs%d" % u) for u in range(2)]
         by_scalar = tile([P, T], F32, "by_scalar")
         by_vector = tile([P, T], F32, "by_vector")
@@ -147,24 +147,24 @@ def tile_moe_hie_none_kernel(tc, x_words, x_scales, wg, we_words, we_scales, gat
         def work_runs(first):
             return work[:, first * C2 : (first + 2) * C2]
 
-        picked1 = tile([P, 2 * C2], U32, "picked1")
-        picked = [work_runs(1).bitcast(U32), picked1[:], work_runs(2).bitcast(U32), work_runs(1).bitcast(U32)]
+        picked = ((2, 3), (8, 9), (3, 4), (1, 3))
         a_bf = {}
         y_banks = {}
         gated = {}
 
         def runs(e):
-            return picked[e]
+            low, high = picked[e]
+            return work[:].bitcast(U32).rearrange("p (r s) -> p s r", s=C2)[:, :, low : high + 1 : high - low]
 
         def gather_pairs(e, u):
             window = pairs[u][:].bitcast(U32)[:, 0 : (e // 2 + 1) * C1]
-            nc.vector.tensor_copy(runs(e)[:, u * C2 : (u + 1) * C2], window.indirect(entries(offs2_t, e * C2, C2)))
+            nc.vector.tensor_copy(work[:, picked[e][u] * C2 : (picked[e][u] + 1) * C2].bitcast(U32), window.indirect(entries(offs2_t, e * C2, C2)))
 
         def join_pairs(e, copy):
-            a_bf[e] = work_runs(0).bitcast(BF16) if e == 1 else tile([P, PACK * C2], BF16, "a_bf%d" % e)[:]
+            a_bf[e] = work_runs(0).bitcast(BF16) if e < 2 else tile([P, PACK * C2], BF16, "a_bf%d" % e)[:]
             copy(
                 a_bf[e].bitcast(U32).rearrange("p (s u) -> p s u", u=2),
-                runs(e).rearrange("p (u s) -> p s u", u=2),
+                runs(e),
             )
 
         def second_level(e, tag=None):
@@ -216,7 +216,7 @@ def tile_moe_hie_none_kernel(tc, x_words, x_scales, wg, we_words, we_scales, gat
         first_level(1, 0, C2)
         join_pairs(0, nc.scalar.copy)
         second_level(0)
-        join_pairs(1, nc.scalar.copy)
+        join_pairs(1, nc.gpsimd.tensor_copy)
         first_level(1, 1, 0)
         first_level(1, 1, C2)
         gather_pairs(2, 0)

@@ -214,7 +214,7 @@ def tile_moe_hie_none_kernel(tc, x_words, x_scales, wg, we_words, we_scales, gat
         gather_pairs(1, 1)
         first_level(1, 0, 0)
         first_level(1, 0, C2)
-        join_pairs(0, nc.scalar.copy)
+        join_pairs(0, nc.gpsimd.tensor_copy)
         second_level(0)
         join_pairs(1, nc.gpsimd.tensor_copy)
         first_level(1, 1, 0)

@@ -25,6 +25,7 @@ HALF = H // 2
 SCALE_SPARE = 384
 SHARED = 256
 PIECES = ((0, 0, 64), (0, 64, 128), (1, 0, 64), (1, 64, 128))
+SHIFT = 0
 A_BANKS, Y_BANKS = 6, 2
 
 
@@ -49,9 +50,9 @@ def tile_moe_hie_none_kernel(tc, x_words, x_scales, wg, we_words, we_scales, gat
         wg_raw = {(f, m0): tile([P, PACK, PACK * (m1 - m0)], F32, "wg_raw%d_%d" % (f, m0)) for f, m0, m1 in PIECES}
         we_w = tile([P, E, 2 * N], U8, "we_w")
         we_s = tile([P, E, N], U8, "we_s")
-        work = tile([P, 6 * C2 + T], F32, "work")
-        gate_t = work[:, 4 * C2 : 4 * C2 + T]
-        pairs = [tile([P, 2 * T], BF16, "pairs%d" % u) for u in range(2)]
+        work = tile([P, 8 * C2 + T], F32, "work")
+        gate_of = [work[:, r * C2 : (r + 1) * C2] for r in (8, 3, 4, 5)]
+        pairs = tile([P, 2 * 2 * T], BF16, "pairs")
         by_scalar = tile([P, T], F32, "by_scalar")
         by_vector = tile([P, T], F32, "by_vector")
         result = tile([P, T], F32, "result")
@@ -81,10 +82,10 @@ def tile_moe_hie_none_kernel(tc, x_words, x_scales, wg, we_words, we_scales, gat
         nc.sync.dma_start(we_w[:].bitcast(I32), we_words[:, 0].rearrange("e p b -> p e b").bitcast(I32))
         for r in range(4):
             if r == 3:
-                nc.sync.dma_start(gate_t[:, 0:C2], gate[:, 0:C2])
+                nc.sync.dma_start(gate_of[0], gate[:, 0:C2])
             nc.sync.dma_start(we_s[r:P:QUADRANT].bitcast(I32), we_scales[:, 0, r:16:4, :].rearrange("e q n -> q e n").bitcast(I32))
 
-        nc.sync.dma_start(gate_t[:, C2:], gate[:, C2:])
+        nc.sync.dma_start(work[:, 3 * C2 : 6 * C2], gate[:, C2:])
         nc.sync.dma_start(dst_t[:], dst)
 
         slot_words = {}
@@ -140,32 +141,39 @@ def tile_moe_hie_none_kernel(tc, x_words, x_scales, wg, we_words, we_scales, gat
                     stop=True,
                 )
             nc.scalar.copy(
-                pairs[u][:].rearrange("p (s d) -> p s d", d=2)[:, first : first + C2, :],
+                pairs[:].rearrange("p (s d) -> p s d", d=2)[:, (2 * f + u) * C1 + c0 : (2 * f + u) * C1 + c0 + C2, :],
                 bank[:].rearrange("p d s -> p s d"),
             )
 
         def work_runs(first):
             return work[:, first * C2 : (first + 2) * C2]
 
-        picked = ((2, 3), (8, 9), (3, 4), (1, 3))
+        picked = ((6 * C2, 7 * C2), (9 * C2, 10 * C2), (6 * C2, 7 * C2 + P), (0, 6 * C2))
         a_bf = {}
         y_banks = {}
-        gated = {}
+        gated = tile([P, T], F32, "gated")
 
         def runs(e):
             low, high = picked[e]
-            return work[:].bitcast(U32).rearrange("p (r s) -> p s r", s=C2)[:, :, low : high + 1 : high - low]
+            return work[:, low : 2 * high - low].bitcast(U32).rearrange("p (u s) -> p s u", u=2)[:, 0:C2]
 
-        def gather_pairs(e, u):
-            window = pairs[u][:].bitcast(U32)[:, 0 : (e // 2 + 1) * C1]
-            nc.vector.tensor_copy(work[:, picked[e][u] * C2 : (picked[e][u] + 1) * C2].bitcast(U32), window.indirect(entries(offs2_t, e * C2, C2)))
+        def gather_pairs(e, u, c0=0, count=C2, run_on=0):
+            f = e // 2
+            window = pairs[:].bitcast(U32)[:, (f + u) * C1 : (2 * f + u + 1 + run_on) * C1]
+            nc.vector.tensor_copy(work[:, picked[e][u] + c0 : picked[e][u] + c0 + count].bitcast(U32), window.indirect(entries(offs2_t, e * C2 + c0, count)))
 
-        def join_pairs(e, copy):
-            a_bf[e] = work_runs(0).bitcast(BF16) if e < 2 else tile([P, PACK * C2], BF16, "a_bf%d" % e)[:]
+        def join_pairs(e, copy, c0=0, count=C2):
+            if c0 == 0:
+                a_bf[e] = work_runs(e // 2).bitcast(BF16) if e < 3 else tile([P, PACK * C2], BF16, "a_bf%d" % e)[:]
             copy(
-                a_bf[e].bitcast(U32).rearrange("p (s u) -> p s u", u=2),
-                runs(e),
+                a_bf[e].bitcast(U32).rearrange("p (s u) -> p s u", u=2)[:, c0 : c0 + count],
+                runs(e)[:, c0 : c0 + count],
             )
+
+        def second_pairs_in_halves(e):
+            for c0 in (0, P):
+                gather_pairs(e, 1, c0, P)
+                join_pairs(e, nc.gpsimd.tensor_copy, c0, P)
 
         def second_level(e, tag=None):
             a_codes = tile([P, C2], U32, "a_codes%d" % e)
@@ -183,14 +191,13 @@ def tile_moe_hie_none_kernel(tc, x_words, x_scales, wg, we_words, we_scales, gat
             )
 
         def apply_gate(e):
-            gated[e] = tile([P, C2], F32, "gated%d" % e)
-            nc.vector.tensor_tensor(gated[e][:], y_banks[e][:], gate_t[:, e * C2 : (e + 1) * C2], MULT)
+            nc.vector.tensor_tensor(gated[:, e * C2 : (e + 1) * C2], y_banks[e][:], gate_of[e], MULT)
 
-        def scatter(e, c0=0, count=C2):
-            nc.scalar.activation(by_scalar[:].indirect(entries(dst_t, e * C2 + c0, count)), gated[e][:, c0 : c0 + count], COPY)
+        def scatter(first, count):
+            nc.scalar.activation(by_scalar[:].indirect(entries(dst_t, first, count)), gated[:, first : first + count], COPY)
 
-        def scatter_on_vector(e, c0, count):
-            nc.vector.tensor_copy(by_vector[:].indirect(entries(dst_t, e * C2 + c0, count)), gated[e][:, c0 : c0 + count])
+        def scatter_on_vector(first, count):
+            nc.vector.tensor_copy(by_vector[:].indirect(entries(dst_t, first, count)), gated[:, first : first + count])
 
         nc.vector.tensor_copy(all_scales[:], token_scales[:].indirect(offs_t[:]))
         gather_words(0, C1 + C2)
@@ -209,35 +216,39 @@ def tile_moe_hie_none_kernel(tc, x_words, x_scales, wg, we_words, we_scales, gat
                 first_level(0, u, c0)
         quantise_wg(1)
         gather_pairs(0, 0)
-        gather_pairs(1, 0)
-        gather_pairs(0, 1)
+        gather_pairs(1, 0, 0, P)
+        second_pairs_in_halves(0)
+        gather_pairs(1, 0, P, P, 1)
         gather_pairs(1, 1)
         first_level(1, 0, 0)
         first_level(1, 0, C2)
-        join_pairs(0, nc.gpsimd.tensor_copy)
         second_level(0)
         join_pairs(1, nc.gpsimd.tensor_copy)
         first_level(1, 1, 0)
         first_level(1, 1, C2)
         gather_pairs(2, 0)
+        gather_pairs(2, 1, 0, P)
         apply_gate(0)
-        scatter(0)
+        scatter(0, C2)
         second_level(1, "a_scales0")
-        gather_pairs(2, 1)
-        join_pairs(2, nc.gpsimd.tensor_copy)
+        join_pairs(2, nc.gpsimd.tensor_copy, 0, P)
+        gather_pairs(2, 1, P, P)
+        join_pairs(2, nc.gpsimd.tensor_copy, P, P)
         gather_pairs(3, 0)
         apply_gate(1)
-        scatter(1)
+        scatter(C2, C2 - SHIFT)
         second_level(2)
-        gather_pairs(3, 1)
-        join_pairs(3, nc.vector.tensor_copy)
+        gather_pairs(3, 1, 0, P)
+        join_pairs(3, nc.gpsimd.tensor_copy, 0, P)
+        gather_pairs(3, 1, P, P)
+        join_pairs(3, nc.vector.tensor_copy, P, P)
         apply_gate(2)
-        scatter(2, 0, P)
+        scatter(2 * C2 + P, P)
         second_level(3)
-        scatter_on_vector(2, P, P)
+        scatter_on_vector(2 * C2 - SHIFT, P + SHIFT)
         apply_gate(3)
-        scatter(3, 0, P)
-        scatter_on_vector(3, P, P)
+        scatter(3 * C2, P)
+        scatter_on_vector(3 * C2 + P, P)
         for c0, c1 in ((0, 256), (256, 512), (512, 768), (768, 1024)):
             nc.vector.tensor_tensor(result[:, c0:c1], by_scalar[:, c0:c1], by_vector[:, c0:c1], ADD)
             nc.sync.dma_start(out[:, c0:c1], result[:, c0:c1])

@@ -22,11 +22,17 @@ PACK = 4
 QUADRANT = 32
 PER_COLUMN = 16
 HALF = H // 2
+M_HALF = P // 2
+HALF_EXPERT = C2 // 2
 SCALE_SPARE = 384
-SHARED = 256
-PIECES = ((0, 0, 64), (0, 64, 128), (1, 0, 64), (1, 64, 128))
-SHIFT = 0
+SHARED = M_HALF * PACK
+STORES = 4
 A_BANKS, Y_BANKS = 6, 2
+
+WORK_RUNS = 12
+GATE_AT = (8 * C2, 3 * C2, 4 * C2, 5 * C2)
+JOINED_AT = (0, 0, C2)
+PICKED_AT = ((6 * C2, 7 * C2), (9 * C2, 10 * C2), (6 * C2, 7 * C2 + HALF_EXPERT), (0, 6 * C2))
 
 
 def tile_moe_hie_none_kernel(tc, x_words, x_scales, wg, we_words, we_scales, gate, offs, offs2, dst, out):
@@ -47,20 +53,19 @@ def tile_moe_hie_none_kernel(tc, x_words, x_scales, wg, we_words, we_scales, gat
         dst_t = tile([P, T // PER_COLUMN], U16, "dst_t")
         token_words = tile([P, T], I32, "token_words")
         token_scales = tile([P, T + SCALE_SPARE], U8, "token_scales")
-        wg_raw = {(f, m0): tile([P, PACK, PACK * (m1 - m0)], F32, "wg_raw%d_%d" % (f, m0)) for f, m0, m1 in PIECES}
+        wg_raw = {(f, h): tile([P, PACK, PACK * M_HALF], F32, "wg_raw%d_%d" % (f, h)) for f in range(G) for h in range(2)}
         we_w = tile([P, E, 2 * N], U8, "we_w")
         we_s = tile([P, E, N], U8, "we_s")
-        work = tile([P, 8 * C2 + T], F32, "work")
-        gate_of = [work[:, r * C2 : (r + 1) * C2] for r in (8, 3, 4, 5)]
+        work = tile([P, WORK_RUNS * C2], F32, "work")
         pairs = tile([P, 2 * 2 * T], BF16, "pairs")
         by_scalar = tile([P, T], F32, "by_scalar")
-        by_vector = tile([P, T], F32, "by_vector")
+        by_both = tile([P, T], F32, "by_both")
         result = tile([P, T], F32, "result")
 
         nc.vector.memset(we_s[:].rearrange("p e n -> p (e n)").bitcast(I32), 0)
         nc.vector.memset(token_scales[:, T:].bitcast(I32), 0)
         nc.vector.memset(by_scalar[:].bitcast(I32), 0)
-        nc.vector.memset(by_vector[:].bitcast(I32), 0)
+        nc.vector.memset(by_both[:].bitcast(I32), 0)
 
         nc.sync.dma_start(offs_t[:], offs)
         for q in range(P // QUADRANT):
@@ -71,21 +76,22 @@ def tile_moe_hie_none_kernel(tc, x_words, x_scales, wg, we_words, we_scales, gat
                 rows.unsqueeze(0).broadcast_to([QUADRANT // 4, 4, T // 4]),
             )
 
-        def load_wg(f, m0, m1):
-            nc.sync.dma_start(wg_raw[f, m0][:], wg[f].rearrange("(p j) c -> p j c", j=PACK)[:, :, PACK * m0 : PACK * m1])
+        def load_wg(f, h):
+            cols = slice(PACK * M_HALF * h, PACK * M_HALF * (h + 1))
+            nc.sync.dma_start(wg_raw[f, h][:], wg[f].rearrange("(p j) c -> p j c", j=PACK)[:, :, cols])
 
-        load_wg(*PIECES[0])
+        load_wg(0, 0)
         nc.sync.dma_start(token_words[:], x_words[0].rearrange("p t d -> p (t d)").bitcast(I32))
-        for piece in PIECES[1:]:
-            load_wg(*piece)
+        load_wg(0, 1)
+        load_wg(1, 0)
+        load_wg(1, 1)
         nc.sync.dma_start(offs2_t[:], offs2)
         nc.sync.dma_start(we_w[:].bitcast(I32), we_words[:, 0].rearrange("e p b -> p e b").bitcast(I32))
         for r in range(4):
             if r == 3:
-                nc.sync.dma_start(gate_of[0], gate[:, 0:C2])
+                nc.sync.dma_start(work[:, GATE_AT[0] : GATE_AT[0] + C2], gate[:, 0:C2])
             nc.sync.dma_start(we_s[r:P:QUADRANT].bitcast(I32), we_scales[:, 0, r:16:4, :].rearrange("e q n -> q e n").bitcast(I32))
-
-        nc.sync.dma_start(work[:, 3 * C2 : 6 * C2], gate[:, C2:])
+        nc.sync.dma_start(work[:, GATE_AT[1] : GATE_AT[1] + T - C2], gate[:, C2:])
         nc.sync.dma_start(dst_t[:], dst)
 
         slot_words = {}
@@ -100,26 +106,24 @@ def tile_moe_hie_none_kernel(tc, x_words, x_scales, wg, we_words, we_scales, gat
             start = max(s for s in slot_words if s <= first)
             return slot_words[start][:, first - start : first - start + C2]
 
-        wg_shared = tile([P, 768 + 2 * H], BF16, "wg_shared")
-        wg_late = tile([P, 768 + 2 * H], BF16, "wg_late")
+        rounded = [tile([P, 4 * H - SHARED], BF16, "rounded%d" % u) for u in range(2)]
         wg_in = [
-            [wg_late[:, 768:], wg_shared[:, 768:]],
-            [wg_shared[:, 0 : 2 * H], wg_late[:, 0 : 2 * H]],
+            [rounded[1][:, 2 * H - SHARED :], rounded[0][:, 2 * H - SHARED :]],
+            [rounded[0][:, 0 : 2 * H], rounded[1][:, 0 : 2 * H]],
         ]
         wg_codes = [tile([P, H], U32, "wg_codes%d" % f) for f in range(G)]
         wg_scales = [tile([P, H], U8, "wg_scales%d" % f) for f in range(G)]
 
-        def views(f, u, m0, m1, walk):
-            start = max(s for g, s, end in PIECES if g == f and s <= m0)
-            target = wg_in[f][u].rearrange("p (t m j) -> p m t j", t=2, j=PACK)[:, m0:m1]
-            source = wg_raw[f, start][:].rearrange("p j (m t) -> p m t j", t=PACK)[:, m0 - start : m1 - start, 2 * u : 2 * u + 2]
-            return target.rearrange("p m t j -> " + walk), source.rearrange("p m t j -> " + walk)
+        def views(f, h, u, walk):
+            target = wg_in[f][u].rearrange("p (d m j) -> p m d j", d=2, j=PACK)[:, M_HALF * h : M_HALF * (h + 1)]
+            source = wg_raw[f, h][:].rearrange("p j (m t) -> p m t j", t=PACK)[:, :, 2 * u : 2 * u + 2]
+            return target.rearrange("p m d j -> " + walk), source.rearrange("p m d j -> " + walk)
 
-        def round_wg(copy, f, u, m0, m1):
-            copy(*views(f, u, m0, m1, "p m j t"))
+        def round_wg(copy, f, h, u):
+            copy(*views(f, h, u, "p m j d"))
 
-        def round_on_gpsimd(f, u, m0, m1):
-            nc.gpsimd.tensor_scalar(*views(f, u, m0, m1, "p m t j"), 1.0, 0.0, MULT, ADD)
+        def round_on_gpsimd(f, h, u):
+            nc.gpsimd.tensor_scalar(*views(f, h, u, "p m d j"), 1.0, 0.0, MULT, ADD)
 
         def quantise_wg(f):
             for u in range(2):
@@ -140,40 +144,39 @@ def tile_moe_hie_none_kernel(tc, x_words, x_scales, wg, we_words, we_scales, gat
                     start=True,
                     stop=True,
                 )
+            word = (2 * f + u) * C1 + c0
             nc.scalar.copy(
-                pairs[:].rearrange("p (s d) -> p s d", d=2)[:, (2 * f + u) * C1 + c0 : (2 * f + u) * C1 + c0 + C2, :],
+                pairs[:].rearrange("p (s d) -> p s d", d=2)[:, word : word + C2, :],
                 bank[:].rearrange("p d s -> p s d"),
             )
 
-        def work_runs(first):
-            return work[:, first * C2 : (first + 2) * C2]
-
-        picked = ((6 * C2, 7 * C2), (9 * C2, 10 * C2), (6 * C2, 7 * C2 + P), (0, 6 * C2))
         a_bf = {}
         y_banks = {}
         gated = tile([P, T], F32, "gated")
 
-        def runs(e):
-            low, high = picked[e]
-            return work[:, low : 2 * high - low].bitcast(U32).rearrange("p (u s) -> p s u", u=2)[:, 0:C2]
-
         def gather_pairs(e, u, c0=0, count=C2, run_on=0):
             f = e // 2
             window = pairs[:].bitcast(U32)[:, (f + u) * C1 : (2 * f + u + 1 + run_on) * C1]
-            nc.vector.tensor_copy(work[:, picked[e][u] + c0 : picked[e][u] + c0 + count].bitcast(U32), window.indirect(entries(offs2_t, e * C2 + c0, count)))
-
-        def join_pairs(e, copy, c0=0, count=C2):
-            if c0 == 0:
-                a_bf[e] = work_runs(e // 2).bitcast(BF16) if e < 3 else tile([P, PACK * C2], BF16, "a_bf%d" % e)[:]
-            copy(
-                a_bf[e].bitcast(U32).rearrange("p (s u) -> p s u", u=2)[:, c0 : c0 + count],
-                runs(e)[:, c0 : c0 + count],
+            first = PICKED_AT[e][u] + c0
+            nc.vector.tensor_copy(
+                work[:, first : first + count].bitcast(U32), window.indirect(entries(offs2_t, e * C2 + c0, count))
             )
 
-        def second_pairs_in_halves(e):
-            for c0 in (0, P):
-                gather_pairs(e, 1, c0, P)
-                join_pairs(e, nc.gpsimd.tensor_copy, c0, P)
+        def join_pairs(e, copy, c0=0, count=C2):
+            if e not in a_bf:
+                if e < len(JOINED_AT):
+                    a_bf[e] = work[:, JOINED_AT[e] : JOINED_AT[e] + 2 * C2].bitcast(BF16)
+                else:
+                    a_bf[e] = tile([P, PACK * C2], BF16, "a_bf%d" % e)[:]
+            low, high = PICKED_AT[e]
+            both = work[:, low : 2 * high - low].bitcast(U32).rearrange("p (u s) -> p s u", u=2)
+            copy(a_bf[e].bitcast(U32).rearrange("p (s u) -> p s u", u=2)[:, c0 : c0 + count], both[:, c0 : c0 + count])
+
+        def gather_half(e, u, half, run_on=0):
+            gather_pairs(e, u, half * HALF_EXPERT, HALF_EXPERT, run_on)
+
+        def join_half(e, copy, half):
+            join_pairs(e, copy, half * HALF_EXPERT, HALF_EXPERT)
 
         def second_level(e, tag=None):
             a_codes = tile([P, C2], U32, "a_codes%d" % e)
@@ -191,34 +194,38 @@ def tile_moe_hie_none_kernel(tc, x_words, x_scales, wg, we_words, we_scales, gat
             )
 
         def apply_gate(e):
-            nc.vector.tensor_tensor(gated[:, e * C2 : (e + 1) * C2], y_banks[e][:], gate_of[e], MULT)
+            gate_e = work[:, GATE_AT[e] : GATE_AT[e] + C2]
+            nc.vector.tensor_tensor(gated[:, e * C2 : (e + 1) * C2], y_banks[e][:], gate_e, MULT)
 
-        def scatter(first, count):
-            nc.scalar.activation(by_scalar[:].indirect(entries(dst_t, first, count)), gated[:, first : first + count], COPY)
+        def scatter_on_scalar(window, first, count):
+            nc.scalar.activation(window[:].indirect(entries(dst_t, first, count)), gated[:, first : first + count], COPY)
 
         def scatter_on_vector(first, count):
-            nc.vector.tensor_copy(by_vector[:].indirect(entries(dst_t, first, count)), gated[:, first : first + count])
+            nc.vector.tensor_copy(by_both[:].indirect(entries(dst_t, first, count)), gated[:, first : first + count])
 
         nc.vector.tensor_copy(all_scales[:], token_scales[:].indirect(offs_t[:]))
         gather_words(0, C1 + C2)
-        round_wg(nc.scalar.copy, 0, 0, 0, 64)
-        round_wg(nc.scalar.copy, 0, 1, 0, 64)
-        round_wg(nc.scalar.copy, 0, 0, 64, 128)
-        round_on_gpsimd(0, 1, 64, 128)
+        round_wg(nc.scalar.copy, 0, 0, 0)
+        round_wg(nc.scalar.copy, 0, 0, 1)
+        round_wg(nc.scalar.copy, 0, 1, 0)
+        round_on_gpsimd(0, 1, 1)
         quantise_wg(0)
-        gather_words(C1 + C2, C2, "wg_raw0_64")
-        round_wg(nc.scalar.copy, 1, 1, 0, 64)
-        round_wg(nc.scalar.copy, 1, 0, 0, 64)
+        gather_words(C1 + C2, C2, "wg_raw0_1")
+        round_wg(nc.scalar.copy, 1, 0, 1)
+        round_wg(nc.scalar.copy, 1, 0, 0)
         for u in range(2):
-            round_wg(nc.vector.tensor_copy, 1, u, 64, 128)
+            round_wg(nc.vector.tensor_copy, 1, 1, u)
         for u in range(2):
             for c0 in (0, C2):
                 first_level(0, u, c0)
         quantise_wg(1)
+
         gather_pairs(0, 0)
-        gather_pairs(1, 0, 0, P)
-        second_pairs_in_halves(0)
-        gather_pairs(1, 0, P, P, 1)
+        gather_half(1, 0, 0)
+        for half in range(2):
+            gather_half(0, 1, half)
+            join_half(0, nc.gpsimd.tensor_copy, half)
+        gather_half(1, 0, 1, run_on=1)
         gather_pairs(1, 1)
         first_level(1, 0, 0)
         first_level(1, 0, C2)
@@ -227,28 +234,31 @@ def tile_moe_hie_none_kernel(tc, x_words, x_scales, wg, we_words, we_scales, gat
         first_level(1, 1, 0)
         first_level(1, 1, C2)
         gather_pairs(2, 0)
-        gather_pairs(2, 1, 0, P)
+        gather_half(2, 1, 0)
         apply_gate(0)
-        scatter(0, C2)
+        scatter_on_scalar(by_both, 0, C2)
+
         second_level(1, "a_scales0")
-        join_pairs(2, nc.gpsimd.tensor_copy, 0, P)
-        gather_pairs(2, 1, P, P)
-        join_pairs(2, nc.gpsimd.tensor_copy, P, P)
+        join_half(2, nc.gpsimd.tensor_copy, 0)
+        gather_half(2, 1, 1)
+        join_half(2, nc.gpsimd.tensor_copy, 1)
         gather_pairs(3, 0)
         apply_gate(1)
-        scatter(C2, C2 - SHIFT)
+        scatter_on_scalar(by_scalar, C2, C2)
+
         second_level(2)
-        gather_pairs(3, 1, 0, P)
-        join_pairs(3, nc.gpsimd.tensor_copy, 0, P)
-        gather_pairs(3, 1, P, P)
-        join_pairs(3, nc.vector.tensor_copy, P, P)
+        for half, copy in enumerate((nc.gpsimd.tensor_copy, nc.vector.tensor_copy)):
+            gather_half(3, 1, half)
+            join_half(3, copy, half)
         apply_gate(2)
-        scatter(2 * C2 + P, P)
+        scatter_on_scalar(by_scalar, 2 * C2 + HALF_EXPERT, HALF_EXPERT)
+
         second_level(3)
-        scatter_on_vector(2 * C2 - SHIFT, P + SHIFT)
+        scatter_on_vector(2 * C2, HALF_EXPERT)
         apply_gate(3)
-        scatter(3 * C2, P)
-        scatter_on_vector(3 * C2 + P, P)
-        for c0, c1 in ((0, 256), (256, 512), (512, 768), (768, 1024)):
-            nc.vector.tensor_tensor(result[:, c0:c1], by_scalar[:, c0:c1], by_vector[:, c0:c1], ADD)
-            nc.sync.dma_start(out[:, c0:c1], result[:, c0:c1])
+        scatter_on_scalar(by_scalar, 3 * C2, HALF_EXPERT)
+        scatter_on_vector(3 * C2 + HALF_EXPERT, HALF_EXPERT)
+        for c0 in range(0, T, T // STORES):
+            cols = slice(c0, c0 + T // STORES)
+            nc.vector.tensor_tensor(result[:, cols], by_scalar[:, cols], by_both[:, cols], ADD)
+            nc.sync.dma_start(out[:, cols], result[:, cols])

@@ -26,13 +26,13 @@ M_HALF = P // 2
 HALF_EXPERT = C2 // 2
 SCALE_SPARE = 384
 SHARED = M_HALF * PACK
-STORES = 4
+STORE_EDGES = (0, 128, 384, 640, 896, 1024)
 A_BANKS, Y_BANKS = 6, 2
 
-WORK_RUNS = 12
-GATE_AT = (8 * C2, 3 * C2, 4 * C2, 5 * C2)
+WORK_RUNS = 13
+GATE_AT = (10 * C2, 3 * C2, 4 * C2, 5 * C2)
 JOINED_AT = (0, 0, C2)
-PICKED_AT = ((6 * C2, 7 * C2), (9 * C2, 10 * C2), (6 * C2, 7 * C2 + HALF_EXPERT), (0, 6 * C2))
+PICKED_AT = ((6 * C2, 9 * C2), (7 * C2, 8 * C2), (6 * C2, 9 * C2 + HALF_EXPERT), (0, 6 * C2))
 
 
 def tile_moe_hie_none_kernel(tc, x_words, x_scales, wg, we_words, we_scales, gate, offs, offs2, dst, out):
@@ -220,8 +220,7 @@ def tile_moe_hie_none_kernel(tc, x_words, x_scales, wg, we_words, we_scales, gat
                 first_level(0, u, c0)
         quantise_wg(1)
 
-        gather_pairs(0, 0)
-        gather_half(1, 0, 0)
+        gather_pairs(0, 0, 0, C2 + HALF_EXPERT)
         for half in range(2):
             gather_half(0, 1, half)
             join_half(0, nc.gpsimd.tensor_copy, half)
@@ -258,7 +257,7 @@ def tile_moe_hie_none_kernel(tc, x_words, x_scales, wg, we_words, we_scales, gat
         apply_gate(3)
         scatter_on_scalar(by_scalar, 3 * C2, HALF_EXPERT)
         scatter_on_vector(3 * C2 + HALF_EXPERT, HALF_EXPERT)
-        for c0 in range(0, T, T // STORES):
-            cols = slice(c0, c0 + T // STORES)
+        for c0, c1 in zip(STORE_EDGES, STORE_EDGES[1:]):
+            cols = slice(c0, c1)
             nc.vector.tensor_tensor(result[:, cols], by_scalar[:, cols], by_both[:, cols], ADD)
             nc.sync.dma_start(out[:, cols], result[:, cols])

@@ -29,10 +29,10 @@ SHARED = M_HALF * PACK
 STORE_EDGES = (0, 128, 384, 640, 896, 1024)
 A_BANKS, Y_BANKS = 6, 2
 
-WORK_RUNS = 13
-GATE_AT = (10 * C2, 3 * C2, 4 * C2, 5 * C2)
-JOINED_AT = (0, 0, C2)
-PICKED_AT = ((6 * C2, 9 * C2), (7 * C2, 8 * C2), (6 * C2, 9 * C2 + HALF_EXPERT), (0, 6 * C2))
+WORK_RUNS = 11
+GATE_AT = (7 * C2, 8 * C2, 9 * C2, 10 * C2)
+JOINED_AT = (0, 0, C2, 2 * C2)
+PICKED_AT = ((3 * C2, 6 * C2), (4 * C2, 5 * C2), (3 * C2, 6 * C2 + HALF_EXPERT), (0, HALF_EXPERT))
 
 
 def tile_moe_hie_none_kernel(tc, x_words, x_scales, wg, we_words, we_scales, gate, offs, offs2, dst, out):
@@ -150,7 +150,7 @@ def tile_moe_hie_none_kernel(tc, x_words, x_scales, wg, we_words, we_scales, gat
                 bank[:].rearrange("p d s -> p s d"),
             )
 
-        a_bf = {}
+        a_bf = [work[:, JOINED_AT[e] : JOINED_AT[e] + 2 * C2].bitcast(BF16) for e in range(E)]
         y_banks = {}
         gated = tile([P, T], F32, "gated")
 
@@ -162,12 +162,14 @@ def tile_moe_hie_none_kernel(tc, x_words, x_scales, wg, we_words, we_scales, gat
                 work[:, first : first + count].bitcast(U32), window.indirect(entries(offs2_t, e * C2 + c0, count))
             )
 
+        def gather_joined(e, u, half):
+            f = e // 2
+            window = pairs[:].bitcast(U32)[:, (f + u) * C1 : (2 * f + u + 1) * C1]
+            c0 = half * HALF_EXPERT
+            place = a_bf[e].bitcast(U32).rearrange("p (s u) -> p s u", u=2)[:, c0 : c0 + HALF_EXPERT, u]
+            nc.vector.tensor_copy(place, window.indirect(entries(offs2_t, e * C2 + c0, HALF_EXPERT)))
+
         def join_pairs(e, copy, c0=0, count=C2):
-            if e not in a_bf:
-                if e < len(JOINED_AT):
-                    a_bf[e] = work[:, JOINED_AT[e] : JOINED_AT[e] + 2 * C2].bitcast(BF16)
-                else:
-                    a_bf[e] = tile([P, PACK * C2], BF16, "a_bf%d" % e)[:]
             low, high = PICKED_AT[e]
             both = work[:, low : 2 * high - low].bitcast(U32).rearrange("p (u s) -> p s u", u=2)
             copy(a_bf[e].bitcast(U32).rearrange("p (s u) -> p s u", u=2)[:, c0 : c0 + count], both[:, c0 : c0 + count])
@@ -241,14 +243,15 @@ def tile_moe_hie_none_kernel(tc, x_words, x_scales, wg, we_words, we_scales, gat
         join_half(2, nc.gpsimd.tensor_copy, 0)
         gather_half(2, 1, 1)
         join_half(2, nc.gpsimd.tensor_copy, 1)
-        gather_pairs(3, 0)
+        gather_half(3, 0, 0)
+        gather_half(3, 1, 0)
         apply_gate(1)
         scatter_on_scalar(by_scalar, C2, C2)
 
         second_level(2)
-        for half, copy in enumerate((nc.gpsimd.tensor_copy, nc.vector.tensor_copy)):
-            gather_half(3, 1, half)
-            join_half(3, copy, half)
+        join_half(3, nc.gpsimd.tensor_copy, 0)
+        for u in range(2):
+            gather_joined(3, u, 1)
         apply_gate(2)
         scatter_on_scalar(by_scalar, 2 * C2 + HALF_EXPERT, HALF_EXPERT)
 

@@ -24,6 +24,7 @@ PER_COLUMN = 16
 HALF = H // 2
 M_HALF = P // 2
 HALF_EXPERT = C2 // 2
+SHIFT = 32
 SCALE_SPARE = 384
 SHARED = M_HALF * PACK
 STORE_EDGES = (0, 128, 384, 640, 896, 1024)
@@ -195,9 +196,10 @@ def tile_moe_hie_none_kernel(tc, x_words, x_scales, wg, we_words, we_scales, gat
                 stop=True,
             )
 
-        def apply_gate(e):
-            gate_e = work[:, GATE_AT[e] : GATE_AT[e] + C2]
-            nc.vector.tensor_tensor(gated[:, e * C2 : (e + 1) * C2], y_banks[e][:], gate_e, MULT)
+        def apply_gate(e, c0=0, count=C2):
+            gate_e = work[:, GATE_AT[e] + c0 : GATE_AT[e] + c0 + count]
+            first = e * C2 + c0
+            nc.vector.tensor_tensor(gated[:, first : first + count], y_banks[e][:, c0 : c0 + count], gate_e, MULT)
 
         def scatter_on_scalar(window, first, count):
             nc.scalar.activation(window[:].indirect(entries(dst_t, first, count)), gated[:, first : first + count], COPY)
@@ -246,7 +248,7 @@ def tile_moe_hie_none_kernel(tc, x_words, x_scales, wg, we_words, we_scales, gat
         gather_half(3, 0, 0)
         gather_half(3, 1, 0)
         apply_gate(1)
-        scatter_on_scalar(by_scalar, C2, C2)
+        scatter_on_scalar(by_scalar, C2, C2 - SHIFT)
 
         second_level(2)
         join_half(3, nc.gpsimd.tensor_copy, 0)
@@ -256,8 +258,9 @@ def tile_moe_hie_none_kernel(tc, x_words, x_scales, wg, we_words, we_scales, gat
         scatter_on_scalar(by_scalar, 2 * C2 + HALF_EXPERT, HALF_EXPERT)
 
         second_level(3)
-        scatter_on_vector(2 * C2, HALF_EXPERT)
-        apply_gate(3)
+        scatter_on_vector(2 * C2 - SHIFT, HALF_EXPERT + SHIFT)
+        for c0 in (HALF_EXPERT, 0):
+            apply_gate(3, c0, HALF_EXPERT)
         scatter_on_scalar(by_scalar, 3 * C2, HALF_EXPERT)
         scatter_on_vector(3 * C2 + HALF_EXPERT, HALF_EXPERT)
         for c0, c1 in zip(STORE_EDGES, STORE_EDGES[1:]):

@@ -24,7 +24,6 @@ PER_COLUMN = 16
 HALF = H // 2
 M_HALF = P // 2
 HALF_EXPERT = C2 // 2
-SHIFT = 32
 SCALE_SPARE = 384
 SHARED = M_HALF * PACK
 STORE_EDGES = (0, 128, 384, 640, 896, 1024)
@@ -248,7 +247,7 @@ def tile_moe_hie_none_kernel(tc, x_words, x_scales, wg, we_words, we_scales, gat
         gather_half(3, 0, 0)
         gather_half(3, 1, 0)
         apply_gate(1)
-        scatter_on_scalar(by_scalar, C2, C2 - SHIFT)
+        scatter_on_scalar(by_scalar, C2, C2)
 
         second_level(2)
         join_half(3, nc.gpsimd.tensor_copy, 0)
@@ -258,7 +257,7 @@ def tile_moe_hie_none_kernel(tc, x_words, x_scales, wg, we_words, we_scales, gat
         scatter_on_scalar(by_scalar, 2 * C2 + HALF_EXPERT, HALF_EXPERT)
 
         second_level(3)
-        scatter_on_vector(2 * C2 - SHIFT, HALF_EXPERT + SHIFT)
+        scatter_on_vector(2 * C2, HALF_EXPERT)
         for c0 in (HALF_EXPERT, 0):
             apply_gate(3, c0, HALF_EXPERT)
         scatter_on_scalar(by_scalar, 3 * C2, HALF_EXPERT)

@@ -27,6 +27,8 @@ HALF_EXPERT = C2 // 2
 SCALE_SPARE = 384
 SHARED = M_HALF * PACK
 STORE_EDGES = (0, 128, 384, 640, 896, 1024)
+WORD_SPARE = 192
+WORDS_AHEAD = 896
 A_BANKS, Y_BANKS = 6, 2
 
 WORK_RUNS = 11
@@ -51,9 +53,10 @@ def tile_moe_hie_none_kernel(tc, x_words, x_scales, wg, we_words, we_scales, gat
         offs_t = tile([P, T // PER_COLUMN], U16, "offs_t")
         offs2_t = tile([P, T // PER_COLUMN], U16, "offs2_t")
         dst_t = tile([P, T // PER_COLUMN], U16, "dst_t")
-        token_words = tile([P, T], I32, "token_words")
+        token_words = tile([P, T + WORD_SPARE], I32, "token_words")
         token_scales = tile([P, T + SCALE_SPARE], U8, "token_scales")
-        wg_raw = {(f, h): tile([P, PACK, PACK * M_HALF], F32, "wg_raw%d_%d" % (f, h)) for f in range(G) for h in range(2)}
+        raw_shape = ([P, 2, H], [P, PACK, PACK * M_HALF])
+        wg_raw = {(f, h): tile(raw_shape[f], F32, "wg_raw%d_%d" % (f, h)) for f in range(G) for h in range(2)}
         we_w = tile([P, E, 2 * N], U8, "we_w")
         we_s = tile([P, E, N], U8, "we_s")
         work = tile([P, WORK_RUNS * C2], F32, "work")
@@ -64,6 +67,7 @@ def tile_moe_hie_none_kernel(tc, x_words, x_scales, wg, we_words, we_scales, gat
 
         nc.vector.memset(we_s[:].rearrange("p e n -> p (e n)").bitcast(I32), 0)
         nc.vector.memset(token_scales[:, T:].bitcast(I32), 0)
+        nc.gpsimd.memset(token_words[:, T:], 0)
         nc.vector.memset(by_scalar[:].bitcast(I32), 0)
         nc.vector.memset(by_both[:].bitcast(I32), 0)
 
@@ -77,11 +81,12 @@ def tile_moe_hie_none_kernel(tc, x_words, x_scales, wg, we_words, we_scales, gat
             )
 
         def load_wg(f, h):
-            cols = slice(PACK * M_HALF * h, PACK * M_HALF * (h + 1))
-            nc.sync.dma_start(wg_raw[f, h][:], wg[f].rearrange("(p j) c -> p j c", j=PACK)[:, :, cols])
+            rows = wg[f].rearrange("(p j) c -> p j c", j=PACK)
+            part = rows[:, 2 * h : 2 * h + 2, :] if f == 0 else rows[:, :, PACK * M_HALF * h : PACK * M_HALF * (h + 1)]
+            nc.sync.dma_start(wg_raw[f, h][:], part)
 
         load_wg(0, 0)
-        nc.sync.dma_start(token_words[:], x_words[0].rearrange("p t d -> p (t d)").bitcast(I32))
+        nc.sync.dma_start(token_words[:, 0:T], x_words[0].rearrange("p t d -> p (t d)").bitcast(I32))
         load_wg(0, 1)
         load_wg(1, 0)
         load_wg(1, 1)
@@ -102,9 +107,9 @@ def tile_moe_hie_none_kernel(tc, x_words, x_scales, wg, we_words, we_scales, gat
             slot_words[first] = tile([P, count], U32, "slot_words%d" % first, tag)
             nc.vector.tensor_copy(slot_words[first][:], token_words[:].bitcast(U32).indirect(entries(offs_t, first, count)))
 
-        def words_of(first):
+        def words_of(first, count):
             start = max(s for s in slot_words if s <= first)
-            return slot_words[start][:, first - start : first - start + C2]
+            return slot_words[start][:, first - start : first - start + count]
 
         rounded = [tile([P, 4 * H - SHARED], BF16, "rounded%d" % u) for u in range(2)]
         wg_in = [
@@ -115,7 +120,8 @@ def tile_moe_hie_none_kernel(tc, x_words, x_scales, wg, we_words, we_scales, gat
         wg_scales = [tile([P, H], U8, "wg_scales%d" % f) for f in range(G)]
 
         def views(f, h, u, walk):
-            target = wg_in[f][u].rearrange("p (d m j) -> p m d j", d=2, j=PACK)[:, M_HALF * h : M_HALF * (h + 1)]
+            target = wg_in[f][u].rearrange("p (d m j) -> p m d j", d=2, j=PACK)
+            target = target[:, :, :, 2 * h : 2 * h + 2] if f == 0 else target[:, M_HALF * h : M_HALF * (h + 1)]
             source = wg_raw[f, h][:].rearrange("p j (m t) -> p m t j", t=PACK)[:, :, 2 * u : 2 * u + 2]
             return target.rearrange("p m d j -> " + walk), source.rearrange("p m d j -> " + walk)
 
@@ -133,17 +139,19 @@ def tile_moe_hie_none_kernel(tc, x_words, x_scales, wg, we_words, we_scales, gat
         def first_level(f, u, c0):
             bank = a_psum.tile([P, 2, C2], F32, name="a_bank")
             first = f * C1 + c0
+            width = C2 if first + C2 <= WORDS_AHEAD else T - WORDS_AHEAD
             for d in range(2):
                 places = slice(P * (2 * u + d), P * (2 * u + d + 1))
-                nc.tensor.matmul_mx(
-                    bank[:, d, :],
-                    lhsT=wg_codes[f][:, places].bitcast(FP8X4),
-                    lhsT_scale=wg_scales[f][:, places],
-                    rhs=words_of(first).bitcast(FP8X4),
-                    rhs_scale=slot_scales[f][:, c0 : c0 + C2],
-                    start=True,
-                    stop=True,
-                )
+                for s in range(0, C2, width):
+                    nc.tensor.matmul_mx(
+                        bank[:, d, s : s + width],
+                        lhsT=wg_codes[f][:, places].bitcast(FP8X4),
+                        lhsT_scale=wg_scales[f][:, places],
+                        rhs=words_of(first + s, width).bitcast(FP8X4),
+                        rhs_scale=slot_scales[f][:, c0 + s : c0 + s + width],
+                        start=True,
+                        stop=True,
+                    )
             word = (2 * f + u) * C1 + c0
             nc.scalar.copy(
                 pairs[:].rearrange("p (s d) -> p s d", d=2)[:, word : word + C2, :],
@@ -207,13 +215,13 @@ def tile_moe_hie_none_kernel(tc, x_words, x_scales, wg, we_words, we_scales, gat
             nc.vector.tensor_copy(by_both[:].indirect(entries(dst_t, first, count)), gated[:, first : first + count])
 
         nc.vector.tensor_copy(all_scales[:], token_scales[:].indirect(offs_t[:]))
-        gather_words(0, C1 + C2)
+        gather_words(0, WORDS_AHEAD)
         round_wg(nc.scalar.copy, 0, 0, 0)
         round_wg(nc.scalar.copy, 0, 0, 1)
         round_wg(nc.scalar.copy, 0, 1, 0)
         round_on_gpsimd(0, 1, 1)
         quantise_wg(0)
-        gather_words(C1 + C2, C2, "wg_raw0_1")
+        gather_words(WORDS_AHEAD, T - WORDS_AHEAD, "wg_raw0_1")
         round_wg(nc.scalar.copy, 1, 0, 1)
         round_wg(nc.scalar.copy, 1, 0, 0)
         for u in range(2):

@@ -65,7 +65,7 @@ def tile_moe_hie_none_kernel(tc, x_words, x_scales, wg, we_words, we_scales, gat
         by_both = tile([P, T], F32, "by_both")
         result = tile([P, T], F32, "result")
 
-        nc.vector.memset(we_s[:].rearrange("p e n -> p (e n)").bitcast(I32), 0)
+        nc.gpsimd.memset(we_s[:].rearrange("p e n -> p (e n)").bitcast(I32), 0)
         nc.vector.memset(token_scales[:, T:].bitcast(I32), 0)
         nc.gpsimd.memset(token_words[:, T:], 0)
         nc.vector.memset(by_scalar[:].bitcast(I32), 0)

@@ -111,25 +111,22 @@ def tile_moe_hie_none_kernel(tc, x_words, x_scales, wg, we_words, we_scales, gat
             start = max(s for s in slot_words if s <= first)
             return slot_words[start][:, first - start : first - start + count]
 
-        rounded = [tile([P, 4 * H - SHARED], BF16, "rounded%d" % u) for u in range(2)]
-        wg_in = [
-            [rounded[1][:, 2 * H - SHARED :], rounded[0][:, 2 * H - SHARED :]],
-            [rounded[0][:, 0 : 2 * H], rounded[1][:, 0 : 2 * H]],
-        ]
+        wg_in = [[tile([P, 2 * H], BF16, "rounded%d_%d" % (f, u))[:] for u in range(2)] for f in range(G)]
         wg_codes = [tile([P, H], U32, "wg_codes%d" % f) for f in range(G)]
         wg_scales = [tile([P, H], U8, "wg_scales%d" % f) for f in range(G)]
 
-        def views(f, h, u, walk):
+        def views(f, h, u, walk, ms):
             target = wg_in[f][u].rearrange("p (d m j) -> p m d j", d=2, j=PACK)
             target = target[:, :, :, 2 * h : 2 * h + 2] if f == 0 else target[:, M_HALF * h : M_HALF * (h + 1)]
-            source = wg_raw[f, h][:].rearrange("p j (m t) -> p m t j", t=PACK)[:, :, 2 * u : 2 * u + 2]
+            target = target[:, ms]
+            source = wg_raw[f, h][:].rearrange("p j (m t) -> p m t j", t=PACK)[:, ms, 2 * u : 2 * u + 2]
             return target.rearrange("p m d j -> " + walk), source.rearrange("p m d j -> " + walk)
 
-        def round_wg(copy, f, h, u):
-            copy(*views(f, h, u, "p m j d"))
+        def round_wg(copy, f, h, u, ms=slice(None)):
+            copy(*views(f, h, u, "p m j d", ms))
 
-        def round_on_gpsimd(f, h, u):
-            nc.gpsimd.tensor_scalar(*views(f, h, u, "p m d j"), 1.0, 0.0, MULT, ADD)
+        def round_on_gpsimd(f, h, u, ms):
+            nc.gpsimd.tensor_scalar(*views(f, h, u, "p m d j", ms), 1.0, 0.0, MULT, ADD)
 
         def quantise_wg(f):
             for u in range(2):
@@ -219,7 +216,8 @@ def tile_moe_hie_none_kernel(tc, x_words, x_scales, wg, we_words, we_scales, gat
         round_wg(nc.scalar.copy, 0, 0, 0)
         round_wg(nc.scalar.copy, 0, 0, 1)
         round_wg(nc.scalar.copy, 0, 1, 0)
-        round_on_gpsimd(0, 1, 1)
+        round_wg(nc.scalar.copy, 0, 1, 1, slice(0, M_HALF))
+        round_on_gpsimd(0, 1, 1, slice(M_HALF, P))
         quantise_wg(0)
         gather_words(WORDS_AHEAD, T - WORDS_AHEAD, "wg_raw0_1")
         round_wg(nc.scalar.copy, 1, 0, 1)

from contextlib import ExitStack

import concourse.mybir as mybir

K, T, G, C1, E, C2, H, N = 512, 1024, 2, 512, 4, 256, 512, 128
FLOPS = 2 * K * H * T + 2 * H * N * T

F32 = mybir.dt.float32
BF16 = mybir.dt.bfloat16
I32 = mybir.dt.int32
U32 = mybir.dt.uint32
U16 = mybir.dt.uint16
U8 = mybir.dt.uint8
FP8X4 = mybir.dt.float8_e4m3fn_x4
FP4X4 = mybir.dt.float4_e2m1fn_x4
MULT = mybir.AluOpType.mult
ADD = mybir.AluOpType.add
COPY = mybir.ActivationFunctionType.Copy

P = 128
PACK = 4
QUADRANT = 32
PER_COLUMN = 16
HALF = H // 2
M_HALF = P // 2
HALF_EXPERT = C2 // 2
SCALE_SPARE = 384
SHARED = M_HALF * PACK
STORE_EDGES = (0, 128, 384, 640, 896, 1024)
WORD_SPARE = 192
WORDS_AHEAD = 896
A_BANKS, Y_BANKS = 6, 2

WORK_RUNS = 11
GATE_AT = (7 * C2, 8 * C2, 9 * C2, 10 * C2)
JOINED_AT = (0, 0, C2, 2 * C2)
PICKED_AT = ((3 * C2, 6 * C2), (4 * C2, 5 * C2), (3 * C2, 6 * C2 + HALF_EXPERT), (0, HALF_EXPERT))


def tile_moe_hie_none_kernel(tc, x_words, x_scales, wg, we_words, we_scales, gate, offs, offs2, dst, out):
    nc = tc.nc
    with ExitStack() as ctx:
        sbuf = ctx.enter_context(tc.tile_pool(name="sbuf", bufs=1))
        a_psum = ctx.enter_context(tc.psum_pool(name="a_psum", bufs=A_BANKS))
        y_psum = ctx.enter_context(tc.psum_pool(name="y_psum", bufs=Y_BANKS))

        def tile(shape, dtype, name, tag=None):
            return sbuf.tile(shape, dtype, name=name, tag=tag or name, align_bytes=64)

        def entries(list_tile, first, count):
            return list_tile[:, first // PER_COLUMN : (first + count) // PER_COLUMN]

        offs_t = tile([P, T // PER_COLUMN], U16, "offs_t")
        offs2_t = tile([P, T // PER_COLUMN], U16, "offs2_t")
        dst_t = tile([P, T // PER_COLUMN], U16, "dst_t")
        token_words = tile([P, T + WORD_SPARE], I32, "token_words")
        token_scales = tile([P, T + SCALE_SPARE], U8, "token_scales")
        raw_shape = ([P, 2, H], [P, PACK, PACK * M_HALF])
        wg_raw = {(f, h): tile(raw_shape[f], F32, "wg_raw%d_%d" % (f, h)) for f in range(G) for h in range(2)}
        we_w = tile([P, E, 2 * N], U8, "we_w")
        we_s = tile([P, E, N], U8, "we_s")
        work = tile([P, WORK_RUNS * C2], F32, "work")
        pairs = tile([P, 2 * 2 * T], BF16, "pairs")
        by_scalar = tile([P, T], F32, "by_scalar")
        by_both = tile([P, T], F32, "by_both")
        result = tile([P, T], F32, "result")

        nc.gpsimd.memset(we_s[:].rearrange("p e n -> p (e n)").bitcast(I32), 0)
        nc.vector.memset(token_scales[:, T:].bitcast(I32), 0)
        nc.gpsimd.memset(token_words[:, T:], 0)
        nc.vector.memset(by_scalar[:].bitcast(I32), 0)
        nc.vector.memset(by_both[:].bitcast(I32), 0)

        nc.sync.dma_start(offs_t[:], offs)
        for q in range(P // QUADRANT):
            queue = nc.sync if q < 2 else nc.scalar
            rows = x_scales[0, 4 * q : 4 * q + 4, :].bitcast(I32)
            queue.dma_start(
                token_scales[QUADRANT * q : QUADRANT * (q + 1), 0:T].bitcast(I32),
                rows.unsqueeze(0).broadcast_to([QUADRANT // 4, 4, T // 4]),
            )

        def load_wg(f, h):
            rows = wg[f].rearrange("(p j) c -> p j c", j=PACK)
            part = rows[:, 2 * h : 2 * h + 2, :] if f == 0 else rows[:, :, PACK * M_HALF * h : PACK * M_HALF * (h + 1)]
            nc.sync.dma_start(wg_raw[f, h][:], part)

        load_wg(0, 0)
        nc.sync.dma_start(token_words[:, 0:T], x_words[0].rearrange("p t d -> p (t d)").bitcast(I32))
        load_wg(0, 1)
        load_wg(1, 0)
        load_wg(1, 1)
        nc.sync.dma_start(offs2_t[:], offs2)
        nc.sync.dma_start(we_w[:].bitcast(I32), we_words[:, 0].rearrange("e p b -> p e b").bitcast(I32))
        for r in range(4):
            if r == 3:
                nc.sync.dma_start(work[:, GATE_AT[0] : GATE_AT[0] + C2], gate[:, 0:C2])
            nc.sync.dma_start(we_s[r:P:QUADRANT].bitcast(I32), we_scales[:, 0, r:16:4, :].rearrange("e q n -> q e n").bitcast(I32))
        nc.sync.dma_start(work[:, GATE_AT[1] : GATE_AT[1] + T - C2], gate[:, C2:])
        nc.sync.dma_start(dst_t[:], dst)

        slot_words = {}
        all_scales = tile([P, T], U8, "slot_scales")
        slot_scales = [all_scales[:, f * C1 : (f + 1) * C1] for f in range(G)]

        def gather_words(first, count, tag=None):
            slot_words[first] = tile([P, count], U32, "slot_words%d" % first, tag)
            nc.vector.tensor_copy(slot_words[first][:], token_words[:].bitcast(U32).indirect(entries(offs_t, first, count)))

        def words_of(first, count):
            start = max(s for s in slot_words if s <= first)
            return slot_words[start][:, first - start : first - start + count]

        wg_in = [[tile([P, 2 * H], BF16, "rounded%d_%d" % (f, u))[:] for u in range(2)] for f in range(G)]
        wg_codes = [tile([P, H], U32, "wg_codes%d" % f) for f in range(G)]
        wg_scales = [tile([P, H], U8, "wg_scales%d" % f) for f in range(G)]

        def views(f, h, u, walk, ms):
            target = wg_in[f][u].rearrange("p (d m j) -> p m d j", d=2, j=PACK)
            target = target[:, :, :, 2 * h : 2 * h + 2] if f == 0 else target[:, M_HALF * h : M_HALF * (h + 1)]
            target = target[:, ms]
            source = wg_raw[f, h][:].rearrange("p j (m t) -> p m t j", t=PACK)[:, ms, 2 * u : 2 * u + 2]
            return target.rearrange("p m d j -> " + walk), source.rearrange("p m d j -> " + walk)

        def round_wg(copy, f, h, u, ms=slice(None)):
            copy(*views(f, h, u, "p m j d", ms))

        def round_on_gpsimd(f, h, u, ms):
            nc.gpsimd.tensor_scalar(*views(f, h, u, "p m d j", ms), 1.0, 0.0, MULT, ADD)

        def quantise_wg(f):
            for u in range(2):
                cols = slice(u * HALF, (u + 1) * HALF)
                nc.vector.quantize_mx(wg_codes[f][:, cols].bitcast(FP8X4), wg_scales[f][:, cols], wg_in[f][u])

        def first_level(f, u, c0):
            bank = a_psum.tile([P, 2, C2], F32, name="a_bank")
            first = f * C1 + c0
            width = C2 if first + C2 <= WORDS_AHEAD else T - WORDS_AHEAD
            for d in range(2):
                places = slice(P * (2 * u + d), P * (2 * u + d + 1))
                for s in range(0, C2, width):
                    nc.tensor.matmul_mx(
                        bank[:, d, s : s + width],
                        lhsT=wg_codes[f][:, places].bitcast(FP8X4),
                        lhsT_scale=wg_scales[f][:, places],
                        rhs=words_of(first + s, width).bitcast(FP8X4),
                        rhs_scale=slot_scales[f][:, c0 + s : c0 + s + width],
                        start=True,
                        stop=True,
                    )
            word = (2 * f + u) * C1 + c0
            nc.scalar.copy(
                pairs[:].rearrange("p (s d) -> p s d", d=2)[:, word : word + C2, :],
                bank[:].rearrange("p d s -> p s d"),
            )

        a_bf = [work[:, JOINED_AT[e] : JOINED_AT[e] + 2 * C2].bitcast(BF16) for e in range(E)]
        y_banks = {}
        gated = tile([P, T], F32, "gated")

        def gather_pairs(e, u, c0=0, count=C2, run_on=0):
            f = e // 2
            window = pairs[:].bitcast(U32)[:, (f + u) * C1 : (2 * f + u + 1 + run_on) * C1]
            first = PICKED_AT[e][u] + c0
            nc.vector.tensor_copy(
                work[:, first : first + count].bitcast(U32), window.indirect(entries(offs2_t, e * C2 + c0, count))
            )

        def gather_joined(e, u, half):
            f = e // 2
            window = pairs[:].bitcast(U32)[:, (f + u) * C1 : (2 * f + u + 1) * C1]
            c0 = half * HALF_EXPERT
            place = a_bf[e].bitcast(U32).rearrange("p (s u) -> p s u", u=2)[:, c0 : c0 + HALF_EXPERT, u]
            nc.vector.tensor_copy(place, window.indirect(entries(offs2_t, e * C2 + c0, HALF_EXPERT)))

        def join_pairs(e, copy, c0=0, count=C2):
            low, high = PICKED_AT[e]
            both = work[:, low : 2 * high - low].bitcast(U32).rearrange("p (u s) -> p s u", u=2)
            copy(a_bf[e].bitcast(U32).rearrange("p (s u) -> p s u", u=2)[:, c0 : c0 + count], both[:, c0 : c0 + count])

        def gather_half(e, u, half, run_on=0):
            gather_pairs(e, u, half * HALF_EXPERT, HALF_EXPERT, run_on)

        def join_half(e, copy, half):
            join_pairs(e, copy, half * HALF_EXPERT, HALF_EXPERT)

        def second_level(e, tag=None):
            a_codes = tile([P, C2], U32, "a_codes%d" % e)
            a_scales = tile([P, C2], U8, "a_scales%d" % e, tag)
            nc.vector.quantize_mx(a_codes[:].bitcast(FP8X4), a_scales[:], a_bf[e])
            y_banks[e] = y_psum.tile([P, C2], F32, name="y_bank")
            nc.tensor.matmul_mx(
                y_banks[e][:],
                lhsT=we_w[:, e, :].bitcast(FP4X4),
                lhsT_scale=we_s[:, e, :],
                rhs=a_codes[:].bitcast(FP8X4),
                rhs_scale=a_scales[:],
                start=True,
                stop=True,
            )

        def apply_gate(e, c0=0, count=C2):
            gate_e = work[:, GATE_AT[e] + c0 : GATE_AT[e] + c0 + count]
            first = e * C2 + c0
            nc.vector.tensor_tensor(gated[:, first : first + count], y_banks[e][:, c0 : c0 + count], gate_e, MULT)

        def scatter_on_scalar(window, first, count):
            nc.scalar.activation(window[:].indirect(entries(dst_t, first, count)), gated[:, first : first + count], COPY)

        def scatter_on_vector(first, count):
            nc.vector.tensor_copy(by_both[:].indirect(entries(dst_t, first, count)), gated[:, first : first + count])

        nc.vector.tensor_copy(all_scales[:], token_scales[:].indirect(offs_t[:]))
        gather_words(0, WORDS_AHEAD)
        round_wg(nc.scalar.copy, 0, 0, 0)
        round_wg(nc.scalar.copy, 0, 0, 1)
        round_wg(nc.scalar.copy, 0, 1, 0)
        round_wg(nc.scalar.copy, 0, 1, 1, slice(0, M_HALF))
        round_on_gpsimd(0, 1, 1, slice(M_HALF, P))
        quantise_wg(0)
        gather_words(WORDS_AHEAD, T - WORDS_AHEAD, "wg_raw0_1")
        round_wg(nc.scalar.copy, 1, 0, 1)
        round_wg(nc.scalar.copy, 1, 0, 0)
        for u in range(2):
            round_wg(nc.vector.tensor_copy, 1, 1, u)
        for u in range(2):
            for c0 in (0, C2):
                first_level(0, u, c0)
        quantise_wg(1)

        gather_pairs(0, 0, 0, C2 + HALF_EXPERT)
        for half in range(2):
            gather_half(0, 1, half)
            join_half(0, nc.gpsimd.tensor_copy, half)
        gather_half(1, 0, 1, run_on=1)
        gather_pairs(1, 1)
        first_level(1, 0, 0)
        first_level(1, 0, C2)
        second_level(0)
        join_pairs(1, nc.gpsimd.tensor_copy)
        first_level(1, 1, 0)
        first_level(1, 1, C2)
        gather_pairs(2, 0)
        gather_half(2, 1, 0)
        apply_gate(0)
        scatter_on_scalar(by_both, 0, C2)

        second_level(1, "a_scales0")
        join_half(2, nc.gpsimd.tensor_copy, 0)
        gather_half(2, 1, 1)
        join_half(2, nc.gpsimd.tensor_copy, 1)
        gather_half(3, 0, 0)
        gather_half(3, 1, 0)
        apply_gate(1)
        scatter_on_scalar(by_scalar, C2, C2)

        second_level(2)
        join_half(3, nc.gpsimd.tensor_copy, 0)
        for u in range(2):
            gather_joined(3, u, 1)
        apply_gate(2)
        scatter_on_scalar(by_scalar, 2 * C2 + HALF_EXPERT, HALF_EXPERT)

        second_level(3)
        scatter_on_vector(2 * C2, HALF_EXPERT)
        for c0 in (HALF_EXPERT, 0):
            apply_gate(3, c0, HALF_EXPERT)
        scatter_on_scalar(by_scalar, 3 * C2, HALF_EXPERT)
        scatter_on_vector(3 * C2 + HALF_EXPERT, HALF_EXPERT)
        for c0, c1 in zip(STORE_EDGES, STORE_EDGES[1:]):
            cols = slice(c0, c1)
            nc.vector.tensor_tensor(result[:, cols], by_scalar[:, cols], by_both[:, cols], ADD)
            nc.sync.dma_start(out[:, cols], result[:, cols])
